import numpy as np
import ml_dtypes


def mxq(x, axis, fmt="e4m3"):
    dtype, down = {"e4m3": (ml_dtypes.float8_e4m3fn, 7), "e5m2": (ml_dtypes.float8_e5m2, 14)}[fmt]
    v = np.moveaxis(np.asarray(x, np.float32).astype(ml_dtypes.bfloat16).astype(np.float64), axis, -1)
    blocks = v.reshape(v.shape[:-1] + (-1, 32))
    amax = np.abs(blocks).max(-1, keepdims=True)
    byte = np.maximum(np.where(amax > 0, np.frexp(amax)[1] - 1 + 127, 0) - down, 1)
    scale = np.exp2(byte - 127.0)
    codes = (blocks / scale).astype(np.float32).astype(dtype).astype(np.float64)
    return np.moveaxis((codes * scale).reshape(v.shape), -1, axis)


WIDE = False


def mx_kscale(k):
    if not WIDE:
        return np.ones(k)
    levels = np.array([24, -24, 12, -12, 0])
    if k % 512:
        return np.exp2(np.random.permutation(np.resize(levels, k // 32))).repeat(32)
    a = np.empty((k // 512, 16))
    for p in range(k // 512):
        a[p, :8] = np.random.permutation(np.resize(levels, 8))
        for g in range(8):
            far = levels[np.abs(levels - a[p, g]) >= 10]
            a[p, g + 8] = far[np.random.randint(len(far))]
    return np.exp2(a.ravel()).repeat(32)


def f64(x):
    return np.asarray(x).astype(np.float64)


def striped8(idx):
    return np.concatenate([v.reshape(-1, 16).T for v in idx]).astype(np.uint16)


def unstriped8(offs):
    return np.stack([offs[16 * g:16 * g + 16].T.reshape(-1) for g in range(8)]).astype(np.int64)


E2M1 = np.array([0.0, 0.5, 1.0, 1.5, 2.0, 3.0, 4.0, 6.0, -0.0, -0.5, -1.0, -1.5, -2.0, -3.0, -4.0, -6.0])


def pack_weight(w, fmt):
    k, n = w.shape
    w = f64(np.asarray(w, np.float32).astype(ml_dtypes.bfloat16)).reshape(k // 32, 32, n)
    amax = np.abs(w).max(1)
    if fmt == "e4m3":
        byte = np.frexp(amax)[1] - 1 + 127 - 7
    else:
        mant, ex = np.frexp(amax / 6.0)
        byte = np.where(mant > 0.5, ex, ex - 1) + 127
    byte = np.clip(np.where(amax > 0, byte, 1), 1, 254)
    scaled = (w * np.exp2(127.0 - byte)[:, None, :]).reshape(k, n).astype(np.float32)
    by_word = np.ascontiguousarray(scaled.reshape(k // 512, 128, 4, n).transpose(0, 1, 3, 2))
    if fmt == "e4m3":
        words = by_word.astype(ml_dtypes.float8_e4m3fn).view(np.uint8)
    else:
        c = by_word.astype(ml_dtypes.float4_e2m1fn).view(np.uint8) & 0xF
        words = (c[..., 0::2] | (c[..., 1::2] << 4)).reshape(k // 512, 128, 2 * n)
    return np.ascontiguousarray(words), np.ascontiguousarray(byte.astype(np.uint8).reshape(k // 512, 16, n))


def unpack_weight(words, scales, fmt):
    g, _, n = scales.shape
    words = np.ascontiguousarray(words).reshape(g, 128, n, -1)
    if fmt == "e4m3":
        vals = words.view(ml_dtypes.float8_e4m3fn).astype(np.float64)
    else:
        nib = np.empty((g, 128, n, 4), np.uint8)
        nib[..., 0::2] = words & 0xF
        nib[..., 1::2] = words >> 4
        vals = E2M1[nib]
    vals = vals * np.repeat(np.exp2(scales.astype(np.float64) - 127.0), 8, axis=1)[..., None]
    return vals.transpose(0, 1, 3, 2).reshape(g * 512, n)


def gelu(f):
    return 0.5 * f * (1.0 + np.tanh(np.sqrt(2.0 / np.pi) * (f + 0.044715 * f**3)))


K, R, N, T, J = 1024, 512, 512, 2048, 1024


def setup_inputs():
    n = np.random.standard_normal
    s = mx_kscale(K)[:, None]
    u = mx_kscale(R)[:, None]
    p_wg = pack_weight(n((K, R)) / np.sqrt(K) / s, "e4m3")
    p_wu = pack_weight(n((K, R)) / np.sqrt(K) / s * u.T, "e4m3")
    p_wd = pack_weight(n((R, N)) / np.sqrt(R) / u, "e2m1")
    return {
        "xT": (n((K, T)) * s).astype(np.float32),
        "wgt": np.repeat(np.random.uniform(0.5, 2.0, (8, J)), 16, axis=0).astype(np.float32),
        "wg_words": p_wg[0],
        "wg_scales": p_wg[1],
        "wu_words": p_wu[0],
        "wu_scales": p_wu[1],
        "wd_words": p_wd[0],
        "wd_scales": p_wd[1],
        "b": (0.3 * n(N)).astype(np.float32),
        "wgo": np.repeat(np.random.uniform(0.5, 2.0, (8, J)), 16, axis=0).astype(np.float32),
        "offs": striped8(np.stack([np.random.permutation(T)[:J] for _ in range(8)])),
        "offs2": striped8(np.stack([np.random.permutation(T)[:J] for _ in range(8)])),
    }


def reference(xT, wgt, wg_words, wg_scales, wu_words, wu_scales, wd_words, wd_scales, b, wgo, offs, offs2):
    idx = unstriped8(offs)
    idx2 = unstriped8(offs2)
    rows = np.arange(K)
    xg = f64(wgt)[rows // 4 % 128] * f64(xT)[rows[:, None], idx[rows % 512 // 64]]
    xT_ = mxq(xg, 0, "e4m3")
    wg_ = unpack_weight(wg_words, wg_scales, "e4m3")
    wu_ = unpack_weight(wu_words, wu_scales, "e4m3")
    ga = wg_.T @ xT_
    ub = wu_.T @ xT_
    h = gelu(ga) * ub
    h_ = mxq(h, 0, "e4m3")
    wd_ = unpack_weight(wd_words, wd_scales, "e2m1")
    y = wd_.T @ h_
    out = np.zeros((N, T))
    rows = np.arange(N)
    out[rows[:, None], idx2[rows % 128 // 16]] = f64(wgo)[rows % 128] * (y + f64(b)[:, None])
    return out

@@ -1,0 +1,280 @@
+from contextlib import ExitStack
+
+import concourse.mybir as mybir
+from concourse.masks import make_identity
+
+K, R, N, T, J = 1024, 512, 512, 2048, 1024
+FLOPS = 2 * J * (2 * K * R + R * N)
+
+F32 = mybir.dt.float32
+BF16 = mybir.dt.bfloat16
+I32 = mybir.dt.int32
+U16 = mybir.dt.uint16
+U8 = mybir.dt.uint8
+FP8X4 = mybir.dt.float8_e4m3fn_x4
+FP4X4 = mybir.dt.float4_e2m1fn_x4
+MULT = mybir.AluOpType.mult
+GELU = mybir.ActivationFunctionType.Gelu_apprx_tanh
+IDENTITY = mybir.ActivationFunctionType.Identity
+
+P = 128
+PACK = 4
+PASSES = K // (P * PACK)
+HALF = J // 2
+CHUNK = 128
+CHUNKS = HALF // CHUNK
+N_TILES = N // P
+LANES = 16
+
+
+def tile_list_gelu_scatb_kernel(
+    tc, xT, wgt, wg_words, wg_scales, wu_words, wu_scales, wd_words, wd_scales, b, wgo, offs, offs2, out
+):
+    nc = tc.nc
+    with ExitStack() as ctx:
+        keep = ctx.enter_context(tc.tile_pool(name="keep", bufs=1))
+        psum = ctx.enter_context(tc.psum_pool(name="psum", bufs=1))
+
+        def held(name, shape, dtype, bufs=1, after=None):
+            return keep.tile(shape, dtype, name=name, tag=after or name, bufs=bufs, align_bytes=64)
+
+        def bank(index, shape):
+            return psum.tile(shape, F32, name="bank%d" % index, tag="bank%d" % index)
+
+        picks = held("picks", [P, J // LANES], U16)
+        places = held("places", [P, J // LANES], U16)
+        planes = [held("plane%d" % s, [P, T], F32) for s in range(PASSES * PACK)]
+        windows = [held("window%d" % t, [P, T], F32) for t in range(N_TILES)]
+        wgt_sb = [held("wgt_sb%d" % h, [P, HALF], F32) for h in range(2)]
+        wgo_sb = held("wgo_sb", [P, J], F32)
+        bias = held("bias", [P, N_TILES], F32)
+        w_codes = [[held("w_codes%d%d" % (m, a), [P, R], I32) for a in range(PASSES)] for m in range(2)]
+        w_scale = [held("w_scale%d" % m, [P, PASSES, R], U8) for m in range(2)]
+        wd_codes = held("wd_codes", [P, 2 * N], U8)
+        wd_scale = held("wd_scale", [P, N], U8)
+        ident = held("ident", [P, P], F32)
+        warm_in = held("warm_in", [P, 1], F32)
+        warm_out = held("warm_out", [P, 1], F32)
+        picked = {}
+        x_codes = {}
+        grouped = [[held("grouped%d%d" % (a, h), [P, HALF, PACK], BF16) for h in range(2)] for a in range(PASSES)]
+        x_scale = [[held("x_scale%d%d" % (a, h), [P, HALF], U8) for h in range(2)] for a in range(PASSES)]
+        h_grouped = [held("h_grouped%d" % h, [P, HALF, PACK], BF16) for h in range(2)]
+        h_codes = [held("h_codes%d" % h, [P, HALF], I32) for h in range(2)]
+        h_scale = [held("h_scale%d" % h, [P, HALF], U8) for h in range(2)]
+        y_sb = [[held("y%d%d" % (h, t), [P, HALF], F32) for t in range(N_TILES)] for h in range(2)]
+
+        nc.gpsimd.memset(warm_in[:], 0.0)
+        nc.scalar.activation(warm_out[:], warm_in[:], GELU)
+        make_identity(nc, ident[:])
+        for plane_tile in (w_scale[0], w_scale[1], wd_scale):
+            nc.gpsimd.memset(plane_tile[:].bitcast(I32), 0)
+        for t in range(N_TILES):
+            nc.gpsimd.memset(windows[t][:], 0.0)
+
+        def load_plane(s):
+            a, i = divmod(s, PACK)
+            rows = xT[P * PACK * a : P * PACK * (a + 1), :].rearrange("(p i) t -> p i t", i=PACK)
+            nc.sync.dma_start(planes[s][:], rows[:, i, :])
+
+        def load_scales(dst, src, q):
+            nc.sync.dma_start(
+                dst[32 * q : 32 * q + 4, :, :].bitcast(I32),
+                src.bitcast(I32)[:, 4 * q : 4 * q + 4, :].rearrange("a q n -> q a n"),
+            )
+
+        def load_words(m, a):
+            words = (wg_words, wu_words)[m]
+            nc.sync.dma_start(w_codes[m][a][:], words[a].rearrange("p r i -> p (r i)").bitcast(I32))
+
+        nc.sync.dma_start(picks[:], offs)
+        nc.sync.dma_start(wgt_sb[0][:], wgt[:, :HALF])
+        load_plane(0)
+        nc.sync.dma_start(wgt_sb[1][:], wgt[:, HALF:])
+        for q in range(4):
+            load_plane(1 + q)
+            load_scales(w_scale[0], wg_scales, q)
+            load_scales(w_scale[1], wu_scales, q)
+        load_words(0, 0)
+        load_words(1, 0)
+        for s in range(5, 8):
+            load_plane(s)
+        load_words(0, 1)
+        load_words(1, 1)
+        nc.sync.dma_start(wd_codes[:].bitcast(I32), wd_words[0].bitcast(I32))
+        for q in range(4):
+            nc.sync.dma_start(
+                wd_scale[32 * q : 32 * q + 4, :].bitcast(I32), wd_scales[0].bitcast(I32)[4 * q : 4 * q + 4, :]
+            )
+        with nc.allow_non_contiguous_dma(reason="one bias value a partition and output tile"):
+            nc.sync.dma_start(bias[:], b.rearrange("(t p) -> p t", p=P))
+        nc.sync.dma_start(places[:], offs2)
+        nc.sync.dma_start(wgo_sb[:, :HALF], wgo[:, :HALF])
+        nc.sync.dma_start(wgo_sb[:, HALF:], wgo[:, HALF:])
+
+        def gather(s, h, c0, c1):
+            a, i = divmod(s, PACK)
+            j0, j1 = h * HALF + c0, h * HALF + c1
+            nc.vector.tensor_tensor(
+                picked[a, h, i // 2][:, i % 2, c0:c1],
+                planes[s][:].indirect(picks[:, j0 // LANES : j1 // LANES]),
+                wgt_sb[h][:, c0:c1],
+                MULT,
+            )
+
+        def interleave(a, h, u, c0, c1):
+            nc.scalar.copy(
+                grouped[a][h][:, c0:c1, 2 * u : 2 * u + 2],
+                picked[a, h, u][:, :, c0:c1].rearrange("p i j -> p j i"),
+            )
+
+        def quantize_x(a, h, c0, c1):
+            nc.vector.quantize_mx(
+                out=x_codes[a, h][:, c0:c1].bitcast(FP8X4),
+                scales=x_scale[a][h][:, c0:c1],
+                in_=grouped[a][h][:, c0:c1, :].rearrange("p j i -> p (j i)"),
+            )
+
+        def first_layer(acc, m, a, h, c):
+            j0 = c * CHUNK
+            nc.tensor.matmul_mx(
+                out=acc[:],
+                lhsT=x_codes[a, h][:, j0 : j0 + CHUNK].bitcast(FP8X4),
+                lhsT_scale=x_scale[a][h][:, j0 : j0 + CHUNK],
+                rhs=w_codes[m][a][:].bitcast(FP8X4),
+                rhs_scale=w_scale[m][:, a, :],
+                start=(a == 0),
+                stop=(a == PASSES - 1),
+            )
+
+        def by_word(acc):
+            return acc[:].rearrange("j (p u e) -> j u p e", u=2, e=2)
+
+        def gate(ga):
+            act = held("act", [P, R], F32, bufs=4)
+            nc.scalar.activation(act[:].rearrange("j (u p e) -> j u p e", u=2, e=2), by_word(ga), GELU)
+            return act
+
+        def product(act, ub):
+            hid = held("hid", [P, R], BF16, bufs=4)
+            nc.vector.tensor_tensor(
+                hid[:].rearrange("j (u p e) -> j u p e", u=2, e=2),
+                by_word(ub),
+                act[:].rearrange("j (u p e) -> j u p e", u=2, e=2),
+                MULT,
+            )
+            return hid
+
+        def turn(hid, index):
+            turned = bank(index, [P, 2, CHUNK])
+            words = hid[:].bitcast(F32)
+            for u in range(2):
+                nc.tensor.transpose(turned[:, u, :], words[:, u * P : (u + 1) * P], ident[:])
+            return turned
+
+        def collect(turned, h, c):
+            dst = h_grouped[h][:, c * CHUNK : (c + 1) * CHUNK, :].bitcast(F32)
+            nc.scalar.copy(dst, turned[:].rearrange("p u j -> p j u"))
+
+        def quantize_h(h, c0, c1):
+            nc.vector.quantize_mx(
+                out=h_codes[h][:, c0:c1].bitcast(FP8X4),
+                scales=h_scale[h][:, c0:c1],
+                in_=h_grouped[h][:, c0:c1, :].rearrange("p j i -> p (j i)"),
+            )
+
+        def second_layer(acc, h, t, c0, c1):
+            nc.tensor.matmul_mx(
+                out=acc[:, c0:c1],
+                lhsT=wd_codes[:, 2 * P * t : 2 * P * (t + 1)].bitcast(FP4X4),
+                lhsT_scale=wd_scale[:, P * t : P * (t + 1)],
+                rhs=h_codes[h][:, c0:c1].bitcast(FP8X4),
+                rhs_scale=h_scale[h][:, c0:c1],
+                start=True,
+                stop=True,
+            )
+
+        def add_bias(acc, h, t, c0, c1):
+            nc.scalar.activation(y_sb[h][t][:, c0:c1], acc[:, c0:c1], IDENTITY, bias=bias[:, t : t + 1])
+
+        def whole_tile(h, t, index):
+            acc = bank(index, [P, HALF])
+            second_layer(acc, h, t, 0, HALF)
+            add_bias(acc, h, t, 0, HALF)
+
+        def scatter(h, t):
+            j0, j1 = h * HALF, (h + 1) * HALF
+            nc.vector.tensor_tensor(
+                windows[t][:].indirect(places[:, j0 // LANES : j1 // LANES]),
+                y_sb[h][t][:],
+                wgo_sb[:, j0:j1],
+                MULT,
+            )
+
+        last = PASSES * PACK - 1
+        spans = [(c * CHUNK, (c + 1) * CHUNK) for c in range(CHUNKS)]
+
+        for s in range(last):
+            a, i = divmod(s, PACK)
+            for h in range(2):
+                if (s, h) == (last - 1, 1):
+                    continue
+                if i % 2 == 0:
+                    picked[a, h, i // 2] = held("picked%d%d%d" % (a, h, i // 2), [P, 2, HALF], F32)
+                gather(s, h, 0, HALF)
+                if i % 2 == 1:
+                    interleave(a, h, i // 2, 0, HALF)
+            if s in (PACK, PACK + 1):
+                h = s - PACK
+                x_codes[0, h] = held("x_codes0%d" % h, [P, HALF], I32, after="plane%d" % s)
+                quantize_x(0, h, 0, HALF)
+        for h in range(2):
+            x_codes[1, h] = held("x_codes1%d" % h, [P, HALF], I32)
+        ga = [bank(2 * c, [P, R]) for c in range(CHUNKS)]
+        ub = [bank(2 * c + 1, [P, R]) for c in range(CHUNKS)]
+        for c in range(CHUNKS):
+            first_layer(ga[c], 0, 0, 0, c)
+            first_layer(ub[c], 1, 0, 0, c)
+
+        for c0, c1 in spans:
+            gather(last, 0, c0, c1)
+            interleave(1, 0, 1, c0, c1)
+        for c, (c0, c1) in enumerate(spans):
+            quantize_x(1, 0, c0, c1)
+            first_layer(ga[c], 0, 1, 0, c)
+            first_layer(ub[c], 1, 1, 0, c)
+        acts = [gate(ga[c]) for c in range(CHUNKS)]
+        hids = [product(acts[c], ub[c]) for c in range(CHUNKS)]
+        early, late = bank(1, [P, HALF]), bank(3, [P, HALF])
+        for c, (c0, c1) in enumerate(spans):
+            collect(turn(hids[c], 2 * c), 0, c)
+            quantize_h(0, c0, c1)
+            second_layer(early if c < CHUNKS - 1 else late, 0, 0, c0, c1)
+        add_bias(early, 0, 0, 0, HALF - CHUNK)
+        add_bias(late, 0, 0, HALF - CHUNK, HALF)
+
+        picked[1, 1, 1] = held("picked111", [P, 2, HALF], F32, after="wgt_sb0")
+        for c0, c1 in spans:
+            gather(last - 1, 1, c0, c1)
+            gather(last, 1, c0, c1)
+            interleave(1, 1, 1, c0, c1)
+        for c, (g_bank, u_bank) in enumerate(((0, 5), (2, 7), (4, 1), (6, 3))):
+            quantize_x(1, 1, spans[c][0], spans[c][1])
+            g_acc = bank(g_bank, [P, R])
+            u_acc = bank(u_bank, [P, R])
+            for m, acc in enumerate((g_acc, u_acc)):
+                for a in range(PASSES):
+                    first_layer(acc, m, a, 1, c)
+            collect(turn(product(gate(g_acc), u_acc), u_bank), 1, c)
+        quantize_h(1, 0, HALF)
+        whole_tile(0, 1, 6)
+        whole_tile(0, 2, 3)
+        whole_tile(0, 3, 3)
+        for t, index in enumerate((0, 2, 4, 5)):
+            whole_tile(1, t, index)
+
+        for h in range(2):
+            for t in range(N_TILES):
+                scatter(h, t)
+                if h == 1:
+                    nc.sync.dma_start(out[P * t : P * (t + 1), :], windows[t][:])

@@ -25,6 +25,7 @@ CHUNK = 128
 CHUNKS = HALF // CHUNK
 N_TILES = N // P
 LANES = 16
+SPLIT = 128
 
 
 def tile_list_gelu_scatb_kernel(
@@ -57,20 +58,21 @@ def tile_list_gelu_scatb_kernel(
         warm_out = held("warm_out", [P, 1], F32)
         picked = {}
         x_codes = {}
-        grouped = [[held("grouped%d%d" % (a, h), [P, HALF, PACK], BF16) for h in range(2)] for a in range(PASSES)]
+        grouped = {(a, h): held("grouped%d%d" % (a, h), [P, HALF, PACK], BF16) for a, h in ((0, 0), (0, 1), (1, 0))}
         x_scale = [[held("x_scale%d%d" % (a, h), [P, HALF], U8) for h in range(2)] for a in range(PASSES)]
-        h_grouped = [held("h_grouped%d" % h, [P, HALF, PACK], BF16) for h in range(2)]
+        h_first = [held("h_first%d" % c, [P, CHUNK, PACK], BF16) for c in range(CHUNKS)]
+        h_second = held("h_second", [P, HALF, PACK], BF16)
         h_codes = [held("h_codes%d" % h, [P, HALF], I32) for h in range(2)]
         h_scale = [held("h_scale%d" % h, [P, HALF], U8) for h in range(2)]
-        y_sb = [[held("y%d%d" % (h, t), [P, HALF], F32) for t in range(N_TILES)] for h in range(2)]
+        y_sb = {}
 
         nc.gpsimd.memset(warm_in[:], 0.0)
         nc.scalar.activation(warm_out[:], warm_in[:], GELU)
         make_identity(nc, ident[:])
         for plane_tile in (w_scale[0], w_scale[1], wd_scale):
-            nc.gpsimd.memset(plane_tile[:].bitcast(I32), 0)
+            nc.vector.memset(plane_tile[:].bitcast(I32), 0)
         for t in range(N_TILES):
-            nc.gpsimd.memset(windows[t][:], 0.0)
+            (nc.vector if t < 0 else nc.gpsimd).memset(windows[t][:].bitcast(I32), 0)
 
         def load_plane(s):
             a, i = divmod(s, PACK)
@@ -95,11 +97,12 @@ def tile_list_gelu_scatb_kernel(
             load_plane(1 + q)
             load_scales(w_scale[0], wg_scales, q)
             load_scales(w_scale[1], wu_scales, q)
+        load_plane(5)
+        load_plane(6)
         load_words(0, 0)
-        load_words(1, 0)
-        for s in range(5, 8):
-            load_plane(s)
+        load_plane(7)
         load_words(0, 1)
+        load_words(1, 0)
         load_words(1, 1)
         nc.sync.dma_start(wd_codes[:].bitcast(I32), wd_words[0].bitcast(I32))
         for q in range(4):
@@ -112,11 +115,16 @@ def tile_list_gelu_scatb_kernel(
         nc.sync.dma_start(wgo_sb[:, :HALF], wgo[:, :HALF])
         nc.sync.dma_start(wgo_sb[:, HALF:], wgo[:, HALF:])
 
+        def picked_part(a, h, u, c0, c1):
+            if (a, h, u) in picked:
+                return picked[a, h, u][:, :, c0:c1]
+            return deferred[c0 // CHUNK][:]
+
         def gather(s, h, c0, c1):
             a, i = divmod(s, PACK)
             j0, j1 = h * HALF + c0, h * HALF + c1
             nc.vector.tensor_tensor(
-                picked[a, h, i // 2][:, i % 2, c0:c1],
+                picked_part(a, h, i // 2, c0, c1)[:, i % 2, :],
                 planes[s][:].indirect(picks[:, j0 // LANES : j1 // LANES]),
                 wgt_sb[h][:, c0:c1],
                 MULT,
@@ -124,15 +132,15 @@ def tile_list_gelu_scatb_kernel(
 
         def interleave(a, h, u, c0, c1):
             nc.scalar.copy(
-                grouped[a][h][:, c0:c1, 2 * u : 2 * u + 2],
-                picked[a, h, u][:, :, c0:c1].rearrange("p i j -> p j i"),
+                grouped[a, h][:, c0:c1, 2 * u : 2 * u + 2],
+                picked_part(a, h, u, c0, c1).rearrange("p i j -> p j i"),
             )
 
         def quantize_x(a, h, c0, c1):
             nc.vector.quantize_mx(
                 out=x_codes[a, h][:, c0:c1].bitcast(FP8X4),
                 scales=x_scale[a][h][:, c0:c1],
-                in_=grouped[a][h][:, c0:c1, :].rearrange("p j i -> p (j i)"),
+                in_=grouped[a, h][:, c0:c1, :].rearrange("p j i -> p (j i)"),
             )
 
         def first_layer(acc, m, a, h, c):
@@ -150,13 +158,13 @@ def tile_list_gelu_scatb_kernel(
         def by_word(acc):
             return acc[:].rearrange("j (p u e) -> j u p e", u=2, e=2)
 
-        def gate(ga):
-            act = held("act", [P, R], F32, bufs=4)
+        def gate(ga, c):
+            act = held("act%d" % c, [P, R], F32)
             nc.scalar.activation(act[:].rearrange("j (u p e) -> j u p e", u=2, e=2), by_word(ga), GELU)
             return act
 
-        def product(act, ub):
-            hid = held("hid", [P, R], BF16, bufs=4)
+        def product(act, ub, c):
+            hid = held("hid%d" % c, [P, R], BF16)
             nc.vector.tensor_tensor(
                 hid[:].rearrange("j (u p e) -> j u p e", u=2, e=2),
                 by_word(ub),
@@ -172,15 +180,18 @@ def tile_list_gelu_scatb_kernel(
                 nc.tensor.transpose(turned[:, u, :], words[:, u * P : (u + 1) * P], ident[:])
             return turned
 
+        def h_part(h, c0, c1):
+            return h_second[:, c0:c1, :] if h else h_first[c0 // CHUNK][:]
+
         def collect(turned, h, c):
-            dst = h_grouped[h][:, c * CHUNK : (c + 1) * CHUNK, :].bitcast(F32)
+            dst = h_part(h, c * CHUNK, (c + 1) * CHUNK).bitcast(F32)
             nc.scalar.copy(dst, turned[:].rearrange("p u j -> p j u"))
 
         def quantize_h(h, c0, c1):
             nc.vector.quantize_mx(
                 out=h_codes[h][:, c0:c1].bitcast(FP8X4),
                 scales=h_scale[h][:, c0:c1],
-                in_=h_grouped[h][:, c0:c1, :].rearrange("p j i -> p (j i)"),
+                in_=h_part(h, c0, c1).rearrange("p j i -> p (j i)"),
             )
 
         def second_layer(acc, h, t, c0, c1):
@@ -195,9 +206,10 @@ def tile_list_gelu_scatb_kernel(
             )
 
         def add_bias(acc, h, t, c0, c1):
-            nc.scalar.activation(y_sb[h][t][:, c0:c1], acc[:, c0:c1], IDENTITY, bias=bias[:, t : t + 1])
+            nc.scalar.activation(y_sb[h, t][:, c0:c1], acc[:, c0:c1], IDENTITY, bias=bias[:, t : t + 1])
 
-        def whole_tile(h, t, index):
+        def whole_tile(h, t, index, after=None):
+            y_sb[h, t] = held("y%d%d" % (h, t), [P, HALF], F32, after=after)
             acc = bank(index, [P, HALF])
             second_layer(acc, h, t, 0, HALF)
             add_bias(acc, h, t, 0, HALF)
@@ -206,7 +218,7 @@ def tile_list_gelu_scatb_kernel(
             j0, j1 = h * HALF, (h + 1) * HALF
             nc.vector.tensor_tensor(
                 windows[t][:].indirect(places[:, j0 // LANES : j1 // LANES]),
-                y_sb[h][t][:],
+                y_sb[h, t][:],
                 wgo_sb[:, j0:j1],
                 MULT,
             )
@@ -222,19 +234,16 @@ def tile_list_gelu_scatb_kernel(
                 if i % 2 == 0:
                     picked[a, h, i // 2] = held("picked%d%d%d" % (a, h, i // 2), [P, 2, HALF], F32)
                 gather(s, h, 0, HALF)
-                if i % 2 == 1:
+                if i % 2 == 1 and (a, h) != (1, 1):
                     interleave(a, h, i // 2, 0, HALF)
-            if s in (PACK, PACK + 1):
-                h = s - PACK
-                x_codes[0, h] = held("x_codes0%d" % h, [P, HALF], I32, after="plane%d" % s)
-                quantize_x(0, h, 0, HALF)
-        for h in range(2):
-            x_codes[1, h] = held("x_codes1%d" % h, [P, HALF], I32)
+            if s == 5:
+                x_codes[0, 0] = held("x_codes00", [P, HALF], I32, after="plane%d" % s)
+                quantize_x(0, 0, 0, HALF)
+        x_codes[1, 0] = held("x_codes10", [P, HALF], I32)
         ga = [bank(2 * c, [P, R]) for c in range(CHUNKS)]
         ub = [bank(2 * c + 1, [P, R]) for c in range(CHUNKS)]
         for c in range(CHUNKS):
             first_layer(ga[c], 0, 0, 0, c)
-            first_layer(ub[c], 1, 0, 0, c)
 
         for c0, c1 in spans:
             gather(last, 0, c0, c1)
@@ -242,9 +251,11 @@ def tile_list_gelu_scatb_kernel(
         for c, (c0, c1) in enumerate(spans):
             quantize_x(1, 0, c0, c1)
             first_layer(ga[c], 0, 1, 0, c)
+            first_layer(ub[c], 1, 0, 0, c)
             first_layer(ub[c], 1, 1, 0, c)
-        acts = [gate(ga[c]) for c in range(CHUNKS)]
-        hids = [product(acts[c], ub[c]) for c in range(CHUNKS)]
+        acts = [gate(ga[c], c) for c in range(CHUNKS)]
+        hids = [product(acts[c], ub[c], c) for c in range(CHUNKS)]
+        y_sb[0, 0] = held("y00", [P, HALF], F32)
         early, late = bank(1, [P, HALF]), bank(3, [P, HALF])
         for c, (c0, c1) in enumerate(spans):
             collect(turn(hids[c], 2 * c), 0, c)
@@ -253,28 +264,44 @@ def tile_list_gelu_scatb_kernel(
         add_bias(early, 0, 0, 0, HALF - CHUNK)
         add_bias(late, 0, 0, HALF - CHUNK, HALF)
 
-        picked[1, 1, 1] = held("picked111", [P, 2, HALF], F32, after="wgt_sb0")
+        deferred = [
+            held("deferred%d" % c, [P, 2, CHUNK], F32, after=after)
+            for c, after in enumerate(("wgt_sb0", "grouped10", "h_first2", "h_first3"))
+        ]
         for c0, c1 in spans:
             gather(last - 1, 1, c0, c1)
             gather(last, 1, c0, c1)
+        x_codes[0, 1] = held("x_codes01", [P, HALF], I32, after="plane7")
+        quantize_x(0, 1, 0, HALF)
+        grouped[1, 1] = held("grouped11", [P, HALF, PACK], BF16, after="hid3")
+        for c0 in range(0, HALF, 256):
+            interleave(1, 1, 0, c0, c0 + 256)
+        for c0, c1 in spans:
             interleave(1, 1, 1, c0, c1)
-        for c, (g_bank, u_bank) in enumerate(((0, 5), (2, 7), (4, 1), (6, 3))):
-            quantize_x(1, 1, spans[c][0], spans[c][1])
-            g_acc = bank(g_bank, [P, R])
-            u_acc = bank(u_bank, [P, R])
-            for m, acc in enumerate((g_acc, u_acc)):
-                for a in range(PASSES):
-                    first_layer(acc, m, a, 1, c)
-            collect(turn(product(gate(g_acc), u_acc), u_bank), 1, c)
+        scatter(0, 0)
+        x_codes[1, 1] = held("x_codes11", [P, HALF], I32)
+        quantize_x(1, 1, 0, HALF)
+        whole_tile(0, 1, 7, after="h_first3")
+        banks = ((0, 5), (2, 4), (6, 1), (3, 7))
+        ga = [bank(g_bank, [P, R]) for g_bank, u_bank in banks]
+        ub = [bank(u_bank, [P, R]) for g_bank, u_bank in banks]
+        for a in range(PASSES):
+            for c in range(CHUNKS):
+                first_layer(ga[c], 0, a, 1, c)
+                first_layer(ub[c], 1, a, 1, c)
+        acts = [gate(ga[c], CHUNKS + c) for c in range(CHUNKS)]
+        whole_tile(0, 2, 2)
+        hids = [product(acts[c], ub[c], CHUNKS + c) for c in range(CHUNKS)]
+        for c in range(CHUNKS):
+            collect(turn(hids[c], banks[c][1]), 1, c)
         quantize_h(1, 0, HALF)
-        whole_tile(0, 1, 6)
-        whole_tile(0, 2, 3)
-        whole_tile(0, 3, 3)
-        for t, index in enumerate((0, 2, 4, 5)):
+        whole_tile(0, 3, 7)
+        for t, index in enumerate((0, 3, 6, 5)):
             whole_tile(1, t, index)
 
         for h in range(2):
             for t in range(N_TILES):
-                scatter(h, t)
+                if (h, t) != (0, 0):
+                    scatter(h, t)
                 if h == 1:
                     nc.sync.dma_start(out[P * t : P * (t + 1), :], windows[t][:])

@@ -93,14 +93,22 @@ def tile_list_gelu_scatb_kernel(
         nc.sync.dma_start(wgt_sb[0][:], wgt[:, :HALF])
         load_plane(0)
         nc.sync.dma_start(wgt_sb[1][:], wgt[:, HALF:])
-        for q in range(4):
-            load_plane(1 + q)
-            load_scales(w_scale[0], wg_scales, q)
-            load_scales(w_scale[1], wu_scales, q)
+        load_plane(1)
+        load_plane(2)
+        load_plane(3)
+        load_plane(4)
+        load_scales(w_scale[0], wg_scales, 0)
+        load_scales(w_scale[0], wg_scales, 1)
+        load_scales(w_scale[0], wg_scales, 2)
         load_plane(5)
+        load_scales(w_scale[0], wg_scales, 3)
+        load_scales(w_scale[1], wu_scales, 0)
+        load_scales(w_scale[1], wu_scales, 1)
         load_plane(6)
-        load_words(0, 0)
+        load_scales(w_scale[1], wu_scales, 2)
+        load_scales(w_scale[1], wu_scales, 3)
         load_plane(7)
+        load_words(0, 0)
         load_words(0, 1)
         load_words(1, 0)
         load_words(1, 1)
@@ -115,26 +123,14 @@ def tile_list_gelu_scatb_kernel(
         nc.sync.dma_start(wgo_sb[:, :HALF], wgo[:, :HALF])
         nc.sync.dma_start(wgo_sb[:, HALF:], wgo[:, HALF:])
 
-        def picked_part(a, h, u, c0, c1):
-            if (a, h, u) in picked:
-                return picked[a, h, u][:, :, c0:c1]
-            return deferred[c0 // CHUNK][:]
-
-        def gather(s, h, c0, c1):
-            a, i = divmod(s, PACK)
+        def gather(dst, s, h, c0, c1):
             j0, j1 = h * HALF + c0, h * HALF + c1
             nc.vector.tensor_tensor(
-                picked_part(a, h, i // 2, c0, c1)[:, i % 2, :],
-                planes[s][:].indirect(picks[:, j0 // LANES : j1 // LANES]),
-                wgt_sb[h][:, c0:c1],
-                MULT,
+                dst, planes[s][:].indirect(picks[:, j0 // LANES : j1 // LANES]), wgt_sb[h][:, c0:c1], MULT
             )
 
-        def interleave(a, h, u, c0, c1):
-            nc.scalar.copy(
-                grouped[a, h][:, c0:c1, 2 * u : 2 * u + 2],
-                picked_part(a, h, u, c0, c1).rearrange("p i j -> p j i"),
-            )
+        def interleave(dst, src):
+            nc.scalar.copy(dst, src.rearrange("p i j -> p j i"))
 
         def quantize_x(a, h, c0, c1):
             nc.vector.quantize_mx(
@@ -155,20 +151,17 @@ def tile_list_gelu_scatb_kernel(
                 stop=(a == PASSES - 1),
             )
 
-        def by_word(acc):
-            return acc[:].rearrange("j (p u e) -> j u p e", u=2, e=2)
-
         def gate(ga, c):
             act = held("act%d" % c, [P, R], F32)
-            nc.scalar.activation(act[:].rearrange("j (u p e) -> j u p e", u=2, e=2), by_word(ga), GELU)
+            nc.scalar.activation(act[:], ga[:], GELU)
             return act
 
         def product(act, ub, c):
             hid = held("hid%d" % c, [P, R], BF16)
             nc.vector.tensor_tensor(
-                hid[:].rearrange("j (u p e) -> j u p e", u=2, e=2),
-                by_word(ub),
-                act[:].rearrange("j (u p e) -> j u p e", u=2, e=2),
+                hid[:],
+                ub[:],
+                act[:],
                 MULT,
             )
             return hid
@@ -177,7 +170,7 @@ def tile_list_gelu_scatb_kernel(
             turned = bank(index, [P, 2, CHUNK])
             words = hid[:].bitcast(F32)
             for u in range(2):
-                nc.tensor.transpose(turned[:, u, :], words[:, u * P : (u + 1) * P], ident[:])
+                nc.tensor.transpose(turned[:, u, :], words[:, u : 2 * P : 2], ident[:])
             return turned
 
         def h_part(h, c0, c1):
@@ -226,19 +219,24 @@ def tile_list_gelu_scatb_kernel(
         last = PASSES * PACK - 1
         spans = [(c * CHUNK, (c + 1) * CHUNK) for c in range(CHUNKS)]
 
-        for s in range(last):
-            a, i = divmod(s, PACK)
+        EARLY = 256
+        first_pass = [held("first_pass%d" % h, [P, PACK, HALF], F32) for h in range(2)]
+        for s in range(PACK):
             for h in range(2):
-                if (s, h) == (last - 1, 1):
-                    continue
-                if i % 2 == 0:
-                    picked[a, h, i // 2] = held("picked%d%d%d" % (a, h, i // 2), [P, 2, HALF], F32)
-                gather(s, h, 0, HALF)
-                if i % 2 == 1 and (a, h) != (1, 1):
-                    interleave(a, h, i // 2, 0, HALF)
-            if s == 5:
-                x_codes[0, 0] = held("x_codes00", [P, HALF], I32, after="plane%d" % s)
+                gather(first_pass[h][:, s, :], s, h, 0, HALF)
+        for h in range(2):
+            interleave(grouped[0, h][:], first_pass[h][:])
+        pairs = [held("pair%d" % u, [P, 2, HALF], F32) for u in range(2)]
+        rest = [held("rest0", [P, PACK, EARLY], F32)]
+        for s in range(PACK, last):
+            i = s - PACK
+            gather(pairs[i // 2][:, i % 2, :], s, 0, 0, HALF)
+            gather(rest[0][:, i, :], s, 1, 0, EARLY)
+            if i == 0:
+                x_codes[0, 0] = held("x_codes00", [P, HALF], I32)
                 quantize_x(0, 0, 0, HALF)
+            if i == 1:
+                interleave(grouped[1, 0][:, :, 0:2], pairs[0][:])
         x_codes[1, 0] = held("x_codes10", [P, HALF], I32)
         ga = [bank(2 * c, [P, R]) for c in range(CHUNKS)]
         ub = [bank(2 * c + 1, [P, R]) for c in range(CHUNKS)]
@@ -246,8 +244,8 @@ def tile_list_gelu_scatb_kernel(
             first_layer(ga[c], 0, 0, 0, c)
 
         for c0, c1 in spans:
-            gather(last, 0, c0, c1)
-            interleave(1, 0, 1, c0, c1)
+            gather(pairs[1][:, 1, c0:c1], last, 0, c0, c1)
+            interleave(grouped[1, 0][:, c0:c1, 2:4], pairs[1][:, :, c0:c1])
         for c, (c0, c1) in enumerate(spans):
             quantize_x(1, 0, c0, c1)
             first_layer(ga[c], 0, 1, 0, c)
@@ -264,24 +262,24 @@ def tile_list_gelu_scatb_kernel(
         add_bias(early, 0, 0, 0, HALF - CHUNK)
         add_bias(late, 0, 0, HALF - CHUNK, HALF)
 
-        deferred = [
-            held("deferred%d" % c, [P, 2, CHUNK], F32, after=after)
-            for c, after in enumerate(("wgt_sb0", "grouped10", "h_first2", "h_first3"))
-        ]
-        for c0, c1 in spans:
-            gather(last - 1, 1, c0, c1)
-            gather(last, 1, c0, c1)
-        x_codes[0, 1] = held("x_codes01", [P, HALF], I32, after="plane7")
+        cuts = (0, 256, 384, 512)
+        gather(rest[0][:, PACK - 1, :], last, 1, 0, EARLY)
+        for part, after in enumerate(("pair1", "hid2",), 1):
+            c0, c1 = cuts[part], cuts[part + 1]
+            rest.append(held("rest%d" % part, [P, PACK, c1 - c0], F32, after=after))
+            for i in range(PACK):
+                gather(rest[part][:, i, :], PACK + i, 1, c0, c1)
+        x_codes[0, 1] = held("x_codes01", [P, HALF], I32, after="hid3")
         quantize_x(0, 1, 0, HALF)
-        grouped[1, 1] = held("grouped11", [P, HALF, PACK], BF16, after="hid3")
-        for c0 in range(0, HALF, 256):
-            interleave(1, 1, 0, c0, c0 + 256)
-        for c0, c1 in spans:
-            interleave(1, 1, 1, c0, c1)
+        grouped[1, 1] = held("grouped11", [P, HALF, PACK], BF16, after="h_first3")
+        for part in range(len(rest)):
+            for c0 in range(cuts[part], cuts[part + 1], CHUNK):
+                w0 = c0 - cuts[part]
+                interleave(grouped[1, 1][:, c0 : c0 + CHUNK, :], rest[part][:, :, w0 : w0 + CHUNK])
         scatter(0, 0)
         x_codes[1, 1] = held("x_codes11", [P, HALF], I32)
         quantize_x(1, 1, 0, HALF)
-        whole_tile(0, 1, 7, after="h_first3")
+        whole_tile(0, 1, 7, after="hid2")
         banks = ((0, 5), (2, 4), (6, 1), (3, 7))
         ga = [bank(g_bank, [P, R]) for g_bank, u_bank in banks]
         ub = [bank(u_bank, [P, R]) for g_bank, u_bank in banks]
@@ -295,8 +293,8 @@ def tile_list_gelu_scatb_kernel(
         for c in range(CHUNKS):
             collect(turn(hids[c], banks[c][1]), 1, c)
         quantize_h(1, 0, HALF)
-        whole_tile(0, 3, 7)
-        for t, index in enumerate((0, 3, 6, 5)):
+        whole_tile(0, 3, 0, after="hid7")
+        for t, index in enumerate((3, 6, 2, 5)):
             whole_tile(1, t, index)
 
         for h in range(2):

@@ -47,70 +47,54 @@ def tile_list_gelu_scatb_kernel(
         planes = [held("plane%d" % s, [P, T], F32) for s in range(PASSES * PACK)]
         windows = [held("window%d" % t, [P, T], F32) for t in range(N_TILES)]
         wgt_sb = [held("wgt_sb%d" % h, [P, HALF], F32) for h in range(2)]
-        wgo_sb = held("wgo_sb", [P, J], F32)
+        wgo_sb = [held("wgo_sb%d" % h, [P, HALF], F32) for h in range(2)]
         bias = held("bias", [P, N_TILES], F32)
         w_codes = [[held("w_codes%d%d" % (m, a), [P, R], I32) for a in range(PASSES)] for m in range(2)]
-        w_scale = [held("w_scale%d" % m, [P, PASSES, R], U8) for m in range(2)]
+        w_scale = held("w_scale", [P, R], U8)
         wd_codes = held("wd_codes", [P, 2 * N], U8)
         wd_scale = held("wd_scale", [P, N], U8)
         ident = held("ident", [P, P], F32)
         warm_in = held("warm_in", [P, 1], F32)
         warm_out = held("warm_out", [P, 1], F32)
-        picked = {}
         x_codes = {}
-        grouped = {(a, h): held("grouped%d%d" % (a, h), [P, HALF, PACK], BF16) for a, h in ((0, 0), (0, 1), (1, 0))}
         x_scale = [[held("x_scale%d%d" % (a, h), [P, HALF], U8) for h in range(2)] for a in range(PASSES)]
-        h_first = [held("h_first%d" % c, [P, CHUNK, PACK], BF16) for c in range(CHUNKS)]
-        h_second = held("h_second", [P, HALF, PACK], BF16)
         h_codes = [held("h_codes%d" % h, [P, HALF], I32) for h in range(2)]
         h_scale = [held("h_scale%d" % h, [P, HALF], U8) for h in range(2)]
-        y_sb = {}
 
         nc.gpsimd.memset(warm_in[:], 0.0)
         nc.scalar.activation(warm_out[:], warm_in[:], GELU)
+        nc.gpsimd.memset(w_scale[:].bitcast(I32), 0)
+        nc.gpsimd.memset(wd_scale[:].bitcast(I32), 0)
         make_identity(nc, ident[:])
-        for plane_tile in (w_scale[0], w_scale[1], wd_scale):
-            nc.vector.memset(plane_tile[:].bitcast(I32), 0)
         for t in range(N_TILES):
-            (nc.vector if t < 0 else nc.gpsimd).memset(windows[t][:].bitcast(I32), 0)
+            nc.gpsimd.memset(windows[t][:].bitcast(I32), 0)
+
+        def load_scales(q):
+            for m, scales in enumerate((wg_scales, wu_scales)):
+                p0 = 32 * q + 8 * m
+                nc.sync.dma_start(w_scale[p0 : p0 + 8, :].bitcast(I32), scales.bitcast(I32)[:, 4 * q : 4 * q + 4, :])
 
         def load_plane(s):
             a, i = divmod(s, PACK)
             rows = xT[P * PACK * a : P * PACK * (a + 1), :].rearrange("(p i) t -> p i t", i=PACK)
             nc.sync.dma_start(planes[s][:], rows[:, i, :])
 
-        def load_scales(dst, src, q):
-            nc.sync.dma_start(
-                dst[32 * q : 32 * q + 4, :, :].bitcast(I32),
-                src.bitcast(I32)[:, 4 * q : 4 * q + 4, :].rearrange("a q n -> q a n"),
-            )
-
         def load_words(m, a):
             words = (wg_words, wu_words)[m]
             nc.sync.dma_start(w_codes[m][a][:], words[a].rearrange("p r i -> p (r i)").bitcast(I32))
 
+        last = PASSES * PACK - 1
+        wgt_rows = held("wgt_rows", [P, J // LANES], F32)
+        nc.sync.dma_start(wgt_rows[:], wgt[0:P:LANES, :].rearrange("g (c s) -> g c s", c=LANES))
         nc.sync.dma_start(picks[:], offs)
-        nc.sync.dma_start(wgt_sb[0][:], wgt[:, :HALF])
-        load_plane(0)
-        nc.sync.dma_start(wgt_sb[1][:], wgt[:, HALF:])
-        load_plane(1)
-        load_plane(2)
-        load_plane(3)
-        load_plane(4)
-        load_scales(w_scale[0], wg_scales, 0)
-        load_scales(w_scale[0], wg_scales, 1)
-        load_scales(w_scale[0], wg_scales, 2)
-        load_plane(5)
-        load_scales(w_scale[0], wg_scales, 3)
-        load_scales(w_scale[1], wu_scales, 0)
-        load_scales(w_scale[1], wu_scales, 1)
-        load_plane(6)
-        load_scales(w_scale[1], wu_scales, 2)
-        load_scales(w_scale[1], wu_scales, 3)
-        load_plane(7)
+        for s in range(last):
+            load_plane(s)
+            if 2 <= s < 6:
+                load_scales(s - 2)
         load_words(0, 0)
-        load_words(0, 1)
         load_words(1, 0)
+        load_plane(last)
+        load_words(0, 1)
         load_words(1, 1)
         nc.sync.dma_start(wd_codes[:].bitcast(I32), wd_words[0].bitcast(I32))
         for q in range(4):
@@ -120,8 +104,21 @@ def tile_list_gelu_scatb_kernel(
         with nc.allow_non_contiguous_dma(reason="one bias value a partition and output tile"):
             nc.sync.dma_start(bias[:], b.rearrange("(t p) -> p t", p=P))
         nc.sync.dma_start(places[:], offs2)
-        nc.sync.dma_start(wgo_sb[:, :HALF], wgo[:, :HALF])
-        nc.sync.dma_start(wgo_sb[:, HALF:], wgo[:, HALF:])
+        for h in range(2):
+            nc.sync.dma_start(wgo_sb[h][:], wgo[:, h * HALF : (h + 1) * HALF])
+
+        SQUARE = 32
+        wgt_turned = held("wgt_turned", [P, 2, SQUARE], F32)
+        for u in range(2):
+            nc.vector.transpose(wgt_turned[:, u, :], wgt_rows[:, u * SQUARE : (u + 1) * SQUARE])
+        by_block = wgt_turned[:].rearrange("p u (e c) -> p c u e", e=2)
+        for k in range(4):
+            spread = held("spread%d" % k, [P, 4, 2, 2, LANES], F32)
+            nc.scalar.copy(spread[:], by_block[:, 4 * k : 4 * k + 4].unsqueeze(4).to_broadcast([P, 4, 2, 2, LANES]))
+            c0 = (k % 2) * (HALF // 2)
+            nc.vector.transpose(
+                wgt_sb[k // 2][:, c0 : c0 + HALF // 2], spread[:].rearrange("p c u e r -> p (c u e r)")
+            )
 
         def gather(dst, s, h, c0, c1):
             j0, j1 = h * HALF + c0, h * HALF + c1
@@ -132,12 +129,8 @@ def tile_list_gelu_scatb_kernel(
         def interleave(dst, src):
             nc.scalar.copy(dst, src.rearrange("p i j -> p j i"))
 
-        def quantize_x(a, h, c0, c1):
-            nc.vector.quantize_mx(
-                out=x_codes[a, h][:, c0:c1].bitcast(FP8X4),
-                scales=x_scale[a][h][:, c0:c1],
-                in_=grouped[a, h][:, c0:c1, :].rearrange("p j i -> p (j i)"),
-            )
+        def quantize(codes, scales, grouped):
+            nc.vector.quantize_mx(out=codes.bitcast(FP8X4), scales=scales, in_=grouped.rearrange("p j i -> p (j i)"))
 
         def first_layer(acc, m, a, h, c):
             j0 = c * CHUNK
@@ -146,7 +139,7 @@ def tile_list_gelu_scatb_kernel(
                 lhsT=x_codes[a, h][:, j0 : j0 + CHUNK].bitcast(FP8X4),
                 lhsT_scale=x_scale[a][h][:, j0 : j0 + CHUNK],
                 rhs=w_codes[m][a][:].bitcast(FP8X4),
-                rhs_scale=w_scale[m][:, a, :],
+                rhs_scale=w_scale[8 * m + 4 * a :, :],
                 start=(a == 0),
                 stop=(a == PASSES - 1),
             )
@@ -158,38 +151,21 @@ def tile_list_gelu_scatb_kernel(
 
         def product(act, ub, c):
             hid = held("hid%d" % c, [P, R], BF16)
-            nc.vector.tensor_tensor(
-                hid[:],
-                ub[:],
-                act[:],
-                MULT,
-            )
+            nc.vector.tensor_tensor(hid[:], ub[:], act[:], MULT)
             return hid
 
-        def turn(hid, index):
+        def turn(hid, index, dst):
             turned = bank(index, [P, 2, CHUNK])
             words = hid[:].bitcast(F32)
             for u in range(2):
                 nc.tensor.transpose(turned[:, u, :], words[:, u : 2 * P : 2], ident[:])
-            return turned
+            nc.scalar.copy(dst.bitcast(F32), turned[:].rearrange("p u j -> p j u"))
 
-        def h_part(h, c0, c1):
-            return h_second[:, c0:c1, :] if h else h_first[c0 // CHUNK][:]
-
-        def collect(turned, h, c):
-            dst = h_part(h, c * CHUNK, (c + 1) * CHUNK).bitcast(F32)
-            nc.scalar.copy(dst, turned[:].rearrange("p u j -> p j u"))
-
-        def quantize_h(h, c0, c1):
-            nc.vector.quantize_mx(
-                out=h_codes[h][:, c0:c1].bitcast(FP8X4),
-                scales=h_scale[h][:, c0:c1],
-                in_=h_part(h, c0, c1).rearrange("p j i -> p (j i)"),
-            )
-
-        def second_layer(acc, h, t, c0, c1):
+        def second_layer(h, t, c0, c1, index, after=None, weigh=None):
+            y = held("y%d%d%d" % (h, t, c0), [P, c1 - c0], F32, after=after)
+            acc = bank(index, [P, c1 - c0])
             nc.tensor.matmul_mx(
-                out=acc[:, c0:c1],
+                out=acc[:],
                 lhsT=wd_codes[:, 2 * P * t : 2 * P * (t + 1)].bitcast(FP4X4),
                 lhsT_scale=wd_scale[:, P * t : P * (t + 1)],
                 rhs=h_codes[h][:, c0:c1].bitcast(FP8X4),
@@ -197,109 +173,125 @@ def tile_list_gelu_scatb_kernel(
                 start=True,
                 stop=True,
             )
+            j0, j1 = h * HALF + c0, h * HALF + c1
+            target = windows[t][:].indirect(places[:, j0 // LANES : j1 // LANES])
+            weights = wgo_sb[h][:, c0:c1]
+            if weigh == "vector":
+                nc.vector.scalar_tensor_tensor(y[:], acc[:], bias[:, t : t + 1], weights, mybir.AluOpType.add, MULT)
+                nc.vector.tensor_copy(target, y[:])
+                return
+            nc.scalar.activation(y[:], acc[:], IDENTITY, bias=bias[:, t : t + 1])
+            if weigh == "gpsimd":
+                nc.gpsimd.tensor_tensor(y[:], y[:], weights, MULT)
+                nc.vector.tensor_copy(target, y[:])
+            else:
+                nc.vector.tensor_tensor(target, y[:], weights, MULT)
 
-        def add_bias(acc, h, t, c0, c1):
-            nc.scalar.activation(y_sb[h, t][:, c0:c1], acc[:, c0:c1], IDENTITY, bias=bias[:, t : t + 1])
-
-        def whole_tile(h, t, index, after=None):
-            y_sb[h, t] = held("y%d%d" % (h, t), [P, HALF], F32, after=after)
-            acc = bank(index, [P, HALF])
-            second_layer(acc, h, t, 0, HALF)
-            add_bias(acc, h, t, 0, HALF)
-
-        def scatter(h, t):
-            j0, j1 = h * HALF, (h + 1) * HALF
-            nc.vector.tensor_tensor(
-                windows[t][:].indirect(places[:, j0 // LANES : j1 // LANES]),
-                y_sb[h, t][:],
-                wgo_sb[:, j0:j1],
-                MULT,
-            )
-
-        last = PASSES * PACK - 1
+        QUARTER = HALF // 2
         spans = [(c * CHUNK, (c + 1) * CHUNK) for c in range(CHUNKS)]
 
-        EARLY = 256
         first_pass = [held("first_pass%d" % h, [P, PACK, HALF], F32) for h in range(2)]
+        grouped0 = [held("grouped0%d" % h, [P, HALF, PACK], BF16) for h in range(2)]
         for s in range(PACK):
             for h in range(2):
                 gather(first_pass[h][:, s, :], s, h, 0, HALF)
         for h in range(2):
-            interleave(grouped[0, h][:], first_pass[h][:])
+            interleave(grouped0[h][:], first_pass[h][:])
+
         pairs = [held("pair%d" % u, [P, 2, HALF], F32) for u in range(2)]
-        rest = [held("rest0", [P, PACK, EARLY], F32)]
+        late = [held("late%d" % k, [P, PACK, QUARTER], F32) for k in range(2)]
+        grouped_late = [held("grouped_late%d" % k, [P, QUARTER, PACK], BF16) for k in range(2)]
+        grouped1 = []
+        for c in range(CHUNKS):
+            if c < 2:
+                grouped1.append(late[0][:, 2 + c, :].bitcast(BF16).rearrange("p (j i) -> p j i", i=PACK))
+            else:
+                grouped1.append(held("grouped1%d" % c, [P, CHUNK, PACK], BF16)[:])
         for s in range(PACK, last):
             i = s - PACK
             gather(pairs[i // 2][:, i % 2, :], s, 0, 0, HALF)
-            gather(rest[0][:, i, :], s, 1, 0, EARLY)
-            if i == 0:
-                x_codes[0, 0] = held("x_codes00", [P, HALF], I32)
-                quantize_x(0, 0, 0, HALF)
+            for k in range(2 if i < 2 else 0):
+                gather(late[k][:, i, :], s, 1, k * QUARTER, (k + 1) * QUARTER)
+            if i < 2:
+                x_codes[0, i] = held("x_codes0%d" % i, [P, HALF], I32, after="plane%d" % s)
+                quantize(x_codes[0, i][:], x_scale[0][i][:], grouped0[i][:])
             if i == 1:
-                interleave(grouped[1, 0][:, :, 0:2], pairs[0][:])
-        x_codes[1, 0] = held("x_codes10", [P, HALF], I32)
+                for c, (c0, c1) in enumerate(spans):
+                    interleave(grouped1[c][:, :, 0:2], pairs[0][:, :, c0:c1])
+                for k in range(2):
+                    interleave(grouped_late[k][:, :, 0:2], late[k][:, 0:2, :])
         ga = [bank(2 * c, [P, R]) for c in range(CHUNKS)]
         ub = [bank(2 * c + 1, [P, R]) for c in range(CHUNKS)]
         for c in range(CHUNKS):
             first_layer(ga[c], 0, 0, 0, c)
-
-        for c0, c1 in spans:
-            gather(pairs[1][:, 1, c0:c1], last, 0, c0, c1)
-            interleave(grouped[1, 0][:, c0:c1, 2:4], pairs[1][:, :, c0:c1])
-        for c, (c0, c1) in enumerate(spans):
-            quantize_x(1, 0, c0, c1)
-            first_layer(ga[c], 0, 1, 0, c)
+        for c in range(CHUNKS):
             first_layer(ub[c], 1, 0, 0, c)
+
+        x_codes[1, 0] = held("x_codes10", [P, HALF], I32)
+        for c, (c0, c1) in enumerate(spans):
+            gather(pairs[1][:, 1, c0:c1], last, 0, c0, c1)
+            interleave(grouped1[c][:, :, 2:4], pairs[1][:, :, c0:c1])
+        for c, (c0, c1) in enumerate(spans):
+            quantize(x_codes[1, 0][:, c0:c1], x_scale[1][0][:, c0:c1], grouped1[c])
+            first_layer(ga[c], 0, 1, 0, c)
             first_layer(ub[c], 1, 1, 0, c)
+        for i in (2, 3):
+            gather(late[0][:, i, :], PACK + i, 1, 0, QUARTER)
         acts = [gate(ga[c], c) for c in range(CHUNKS)]
         hids = [product(acts[c], ub[c], c) for c in range(CHUNKS)]
-        y_sb[0, 0] = held("y00", [P, HALF], F32)
-        early, late = bank(1, [P, HALF]), bank(3, [P, HALF])
-        for c, (c0, c1) in enumerate(spans):
-            collect(turn(hids[c], 2 * c), 0, c)
-            quantize_h(0, c0, c1)
-            second_layer(early if c < CHUNKS - 1 else late, 0, 0, c0, c1)
-        add_bias(early, 0, 0, 0, HALF - CHUNK)
-        add_bias(late, 0, 0, HALF - CHUNK, HALF)
+        h_first = [
+            late[1][:, 2:4, :].rearrange("p i j -> p (i j)").bitcast(BF16).rearrange("p (j i) -> p j i", i=PACK),
+            held("h_first1", [P, QUARTER, PACK], BF16)[:],
+        ]
+        for c in range(CHUNKS):
+            turn(hids[c], 2 * c, h_first[c // 2][:, (c % 2) * CHUNK : (c % 2 + 1) * CHUNK, :])
+        for k in range(2):
+            c0, c1 = k * QUARTER, (k + 1) * QUARTER
+            quantize(h_codes[0][:, c0:c1], h_scale[0][:, c0:c1], h_first[k][:])
+            if k == 0:
+                for i in (2, 3):
+                    gather(late[1][:, i, :], PACK + i, 1, QUARTER, HALF)
+        second_layer(0, 0, 0, QUARTER, 1, weigh="vector")
+        second_layer(0, 1, 0, QUARTER, 3, weigh="vector")
 
-        cuts = (0, 256, 384, 512)
-        gather(rest[0][:, PACK - 1, :], last, 1, 0, EARLY)
-        for part, after in enumerate(("pair1", "hid2",), 1):
-            c0, c1 = cuts[part], cuts[part + 1]
-            rest.append(held("rest%d" % part, [P, PACK, c1 - c0], F32, after=after))
-            for i in range(PACK):
-                gather(rest[part][:, i, :], PACK + i, 1, c0, c1)
-        x_codes[0, 1] = held("x_codes01", [P, HALF], I32, after="hid3")
-        quantize_x(0, 1, 0, HALF)
-        grouped[1, 1] = held("grouped11", [P, HALF, PACK], BF16, after="h_first3")
-        for part in range(len(rest)):
-            for c0 in range(cuts[part], cuts[part + 1], CHUNK):
-                w0 = c0 - cuts[part]
-                interleave(grouped[1, 1][:, c0 : c0 + CHUNK, :], rest[part][:, :, w0 : w0 + CHUNK])
-        scatter(0, 0)
         x_codes[1, 1] = held("x_codes11", [P, HALF], I32)
-        quantize_x(1, 1, 0, HALF)
-        whole_tile(0, 1, 7, after="hid2")
-        banks = ((0, 5), (2, 4), (6, 1), (3, 7))
+
+        def late_pass(k):
+            grouped = grouped_late[k]
+            for c0 in range(0, QUARTER, CHUNK):
+                interleave(grouped[:, c0 : c0 + CHUNK, 2:4], late[k][:, 2:4, c0 : c0 + CHUNK])
+            c0, c1 = k * QUARTER, (k + 1) * QUARTER
+            quantize(x_codes[1, 1][:, c0:c1], x_scale[1][1][:, c0:c1], grouped[:])
+
+        late_pass(0)
+        second_layer(0, 2, 0, HALF, 5, weigh="gpsimd")
+        late_pass(1)
+        second_layer(0, 0, QUARTER, HALF, 7, weigh="gpsimd")
+        second_layer(0, 1, QUARTER, HALF, 1, weigh="gpsimd")
+        banks = ((0, 2), (4, 6), (1, 3), (7, 5))
         ga = [bank(g_bank, [P, R]) for g_bank, u_bank in banks]
         ub = [bank(u_bank, [P, R]) for g_bank, u_bank in banks]
         for a in range(PASSES):
             for c in range(CHUNKS):
                 first_layer(ga[c], 0, a, 1, c)
                 first_layer(ub[c], 1, a, 1, c)
-        acts = [gate(ga[c], CHUNKS + c) for c in range(CHUNKS)]
-        whole_tile(0, 2, 2)
-        hids = [product(acts[c], ub[c], CHUNKS + c) for c in range(CHUNKS)]
+        h_second = [held("h_second%d" % k, [P, QUARTER, PACK], BF16) for k in range(2)]
+        hids = []
         for c in range(CHUNKS):
-            collect(turn(hids[c], banks[c][1]), 1, c)
-        quantize_h(1, 0, HALF)
-        whole_tile(0, 3, 0, after="hid7")
-        for t, index in enumerate((3, 6, 2, 5)):
-            whole_tile(1, t, index)
-
-        for h in range(2):
-            for t in range(N_TILES):
-                if (h, t) != (0, 0):
-                    scatter(h, t)
-                if h == 1:
-                    nc.sync.dma_start(out[P * t : P * (t + 1), :], windows[t][:])
+            act = gate(ga[c], CHUNKS + c)
+            up = held("up%d" % c, [P, R], F32, after="plane%d" % c)
+            nc.scalar.copy(up[:], ub[c][:])
+            hid = held("hid%d" % (CHUNKS + c), [P, R], BF16)
+            nc.gpsimd.tensor_tensor(hid[:], up[:], act[:], MULT)
+            hids.append(hid)
+        for k in range(2):
+            for c in (2 * k, 2 * k + 1):
+                turn(hids[c], banks[c][1], h_second[k][:, (c % 2) * CHUNK : (c % 2 + 1) * CHUNK, :])
+            c0, c1 = k * QUARTER, (k + 1) * QUARTER
+            quantize(h_codes[1][:, c0:c1], h_scale[1][:, c0:c1], h_second[k][:])
+            if k == 0:
+                second_layer(0, 3, 0, HALF, 0, after="hid4", weigh="gpsimd")
+        second_layer(1, 0, 0, QUARTER, 4, after="hid7")
+        for t, c0, index in ((1, 0, 1), (0, QUARTER, 7), (2, 0, 2), (3, 0, 6)):
+            second_layer(1, t, c0, HALF, index)
+            nc.sync.dma_start(out[P * t : P * (t + 1), :], windows[t][:])

@@ -46,7 +46,7 @@ def tile_list_gelu_scatb_kernel(
         places = held("places", [P, J // LANES], U16)
         planes = [held("plane%d" % s, [P, T], F32) for s in range(PASSES * PACK)]
         windows = [held("window%d" % t, [P, T], F32) for t in range(N_TILES)]
-        wgt_sb = [held("wgt_sb%d" % h, [P, HALF], F32) for h in range(2)]
+        wgt_sb = held("wgt_sb", [P, J], F32)
         wgo_sb = [held("wgo_sb%d" % h, [P, HALF], F32) for h in range(2)]
         bias = held("bias", [P, N_TILES], F32)
         w_codes = [[held("w_codes%d%d" % (m, a), [P, R], I32) for a in range(PASSES)] for m in range(2)]
@@ -115,15 +115,14 @@ def tile_list_gelu_scatb_kernel(
         for k in range(4):
             spread = held("spread%d" % k, [P, 4, 2, 2, LANES], F32)
             nc.scalar.copy(spread[:], by_block[:, 4 * k : 4 * k + 4].unsqueeze(4).to_broadcast([P, 4, 2, 2, LANES]))
-            c0 = (k % 2) * (HALF // 2)
             nc.vector.transpose(
-                wgt_sb[k // 2][:, c0 : c0 + HALF // 2], spread[:].rearrange("p c u e r -> p (c u e r)")
+                wgt_sb[:, k * J // 4 : (k + 1) * J // 4], spread[:].rearrange("p c u e r -> p (c u e r)")
             )
 
         def gather(dst, s, h, c0, c1):
             j0, j1 = h * HALF + c0, h * HALF + c1
             nc.vector.tensor_tensor(
-                dst, planes[s][:].indirect(picks[:, j0 // LANES : j1 // LANES]), wgt_sb[h][:, c0:c1], MULT
+                dst, planes[s][:].indirect(picks[:, j0 // LANES : j1 // LANES]), wgt_sb[:, j0:j1], MULT
             )
 
         def interleave(dst, src):
@@ -190,36 +189,37 @@ def tile_list_gelu_scatb_kernel(
         QUARTER = HALF // 2
         spans = [(c * CHUNK, (c + 1) * CHUNK) for c in range(CHUNKS)]
 
-        first_pass = [held("first_pass%d" % h, [P, PACK, HALF], F32) for h in range(2)]
+        first_pass = [held("first_pass%d" % u, [P, 2, J], F32) for u in range(2)]
         grouped0 = [held("grouped0%d" % h, [P, HALF, PACK], BF16) for h in range(2)]
         for s in range(PACK):
-            for h in range(2):
-                gather(first_pass[h][:, s, :], s, h, 0, HALF)
-        for h in range(2):
-            interleave(grouped0[h][:], first_pass[h][:])
+            gather(first_pass[s // 2][:, s % 2, :], s, 0, 0, J)
+            if s % 2:
+                for h in range(2):
+                    interleave(grouped0[h][:, :, s - 1 : s + 1], first_pass[s // 2][:, :, h * HALF : (h + 1) * HALF])
 
-        pairs = [held("pair%d" % u, [P, 2, HALF], F32) for u in range(2)]
-        late = [held("late%d" % k, [P, PACK, QUARTER], F32) for k in range(2)]
+        pair_early = held("pair_early", [P, 2, J], F32)
+        pair_last = held("pair_last", [P, 2, HALF], F32)
+        late = [held("late%d" % k, [P, 2, QUARTER], F32) for k in range(2)]
         grouped_late = [held("grouped_late%d" % k, [P, QUARTER, PACK], BF16) for k in range(2)]
         grouped1 = []
         for c in range(CHUNKS):
             if c < 2:
-                grouped1.append(late[0][:, 2 + c, :].bitcast(BF16).rearrange("p (j i) -> p j i", i=PACK))
+                grouped1.append(late[0][:, c, :].bitcast(BF16).rearrange("p (j i) -> p j i", i=PACK))
             else:
                 grouped1.append(held("grouped1%d" % c, [P, CHUNK, PACK], BF16)[:])
-        for s in range(PACK, last):
-            i = s - PACK
-            gather(pairs[i // 2][:, i % 2, :], s, 0, 0, HALF)
-            for k in range(2 if i < 2 else 0):
-                gather(late[k][:, i, :], s, 1, k * QUARTER, (k + 1) * QUARTER)
-            if i < 2:
-                x_codes[0, i] = held("x_codes0%d" % i, [P, HALF], I32, after="plane%d" % s)
-                quantize(x_codes[0, i][:], x_scale[0][i][:], grouped0[i][:])
-            if i == 1:
-                for c, (c0, c1) in enumerate(spans):
-                    interleave(grouped1[c][:, :, 0:2], pairs[0][:, :, c0:c1])
-                for k in range(2):
-                    interleave(grouped_late[k][:, :, 0:2], late[k][:, 0:2, :])
+        gather(pair_early[:, 0, :], PACK, 0, 0, J)
+        x_codes[0, 0] = held("x_codes00", [P, HALF], I32, after="plane4")
+        quantize(x_codes[0, 0][:], x_scale[0][0][:], grouped0[0][:])
+        for h in range(2):
+            gather(pair_early[:, 1, h * HALF : (h + 1) * HALF], PACK + 1, h, 0, HALF)
+        x_codes[0, 1] = held("x_codes01", [P, HALF], I32, after="plane5")
+        quantize(x_codes[0, 1][:], x_scale[0][1][:], grouped0[1][:])
+        for c, (c0, c1) in enumerate(spans):
+            interleave(grouped1[c][:, :, 0:2], pair_early[:, :, c0:c1])
+        for k in range(2):
+            c0 = HALF + k * QUARTER
+            interleave(grouped_late[k][:, :, 0:2], pair_early[:, :, c0 : c0 + QUARTER])
+        gather(pair_last[:, 0, :], last - 1, 0, 0, HALF)
         ga = [bank(2 * c, [P, R]) for c in range(CHUNKS)]
         ub = [bank(2 * c + 1, [P, R]) for c in range(CHUNKS)]
         for c in range(CHUNKS):
@@ -229,18 +229,18 @@ def tile_list_gelu_scatb_kernel(
 
         x_codes[1, 0] = held("x_codes10", [P, HALF], I32)
         for c, (c0, c1) in enumerate(spans):
-            gather(pairs[1][:, 1, c0:c1], last, 0, c0, c1)
-            interleave(grouped1[c][:, :, 2:4], pairs[1][:, :, c0:c1])
+            gather(pair_last[:, 1, c0:c1], last, 0, c0, c1)
+            interleave(grouped1[c][:, :, 2:4], pair_last[:, :, c0:c1])
         for c, (c0, c1) in enumerate(spans):
             quantize(x_codes[1, 0][:, c0:c1], x_scale[1][0][:, c0:c1], grouped1[c])
             first_layer(ga[c], 0, 1, 0, c)
             first_layer(ub[c], 1, 1, 0, c)
         for i in (2, 3):
-            gather(late[0][:, i, :], PACK + i, 1, 0, QUARTER)
+            gather(late[0][:, i - 2, :], PACK + i, 1, 0, QUARTER)
         acts = [gate(ga[c], c) for c in range(CHUNKS)]
         hids = [product(acts[c], ub[c], c) for c in range(CHUNKS)]
         h_first = [
-            late[1][:, 2:4, :].rearrange("p i j -> p (i j)").bitcast(BF16).rearrange("p (j i) -> p j i", i=PACK),
+            late[1][:].rearrange("p i j -> p (i j)").bitcast(BF16).rearrange("p (j i) -> p j i", i=PACK),
             held("h_first1", [P, QUARTER, PACK], BF16)[:],
         ]
         for c in range(CHUNKS):
@@ -250,7 +250,7 @@ def tile_list_gelu_scatb_kernel(
             quantize(h_codes[0][:, c0:c1], h_scale[0][:, c0:c1], h_first[k][:])
             if k == 0:
                 for i in (2, 3):
-                    gather(late[1][:, i, :], PACK + i, 1, QUARTER, HALF)
+                    gather(late[1][:, i - 2, :], PACK + i, 1, QUARTER, HALF)
         second_layer(0, 0, 0, QUARTER, 1, weigh="vector")
         second_layer(0, 1, 0, QUARTER, 3, weigh="vector")
 
@@ -259,7 +259,7 @@ def tile_list_gelu_scatb_kernel(
         def late_pass(k):
             grouped = grouped_late[k]
             for c0 in range(0, QUARTER, CHUNK):
-                interleave(grouped[:, c0 : c0 + CHUNK, 2:4], late[k][:, 2:4, c0 : c0 + CHUNK])
+                interleave(grouped[:, c0 : c0 + CHUNK, 2:4], late[k][:, :, c0 : c0 + CHUNK])
             c0, c1 = k * QUARTER, (k + 1) * QUARTER
             quantize(x_codes[1, 1][:, c0:c1], x_scale[1][1][:, c0:c1], grouped[:])
 

@@ -45,7 +45,6 @@ def tile_list_gelu_scatb_kernel(
         picks = held("picks", [P, J // LANES], U16)
         places = held("places", [P, J // LANES], U16)
         planes = [held("plane%d" % s, [P, T], F32) for s in range(PASSES * PACK)]
-        windows = [held("window%d" % t, [P, T], F32) for t in range(N_TILES)]
         wgt_sb = held("wgt_sb", [P, J], F32)
         wgo_sb = [held("wgo_sb%d" % h, [P, HALF], F32) for h in range(2)]
         bias = held("bias", [P, N_TILES], F32)
@@ -66,8 +65,6 @@ def tile_list_gelu_scatb_kernel(
         nc.gpsimd.memset(w_scale[:].bitcast(I32), 0)
         nc.gpsimd.memset(wd_scale[:].bitcast(I32), 0)
         make_identity(nc, ident[:])
-        for t in range(N_TILES):
-            nc.gpsimd.memset(windows[t][:].bitcast(I32), 0)
 
         def load_scales(q):
             for m, scales in enumerate((wg_scales, wu_scales)):
@@ -92,8 +89,8 @@ def tile_list_gelu_scatb_kernel(
             if 2 <= s < 6:
                 load_scales(s - 2)
         load_words(0, 0)
-        load_words(1, 0)
         load_plane(last)
+        load_words(1, 0)
         load_words(0, 1)
         load_words(1, 1)
         nc.sync.dma_start(wd_codes[:].bitcast(I32), wd_words[0].bitcast(I32))
@@ -114,10 +111,18 @@ def tile_list_gelu_scatb_kernel(
         by_block = wgt_turned[:].rearrange("p u (e c) -> p c u e", e=2)
         for k in range(4):
             spread = held("spread%d" % k, [P, 4, 2, 2, LANES], F32)
-            nc.scalar.copy(spread[:], by_block[:, 4 * k : 4 * k + 4].unsqueeze(4).to_broadcast([P, 4, 2, 2, LANES]))
+            source = by_block[:, 4 * k : 4 * k + 4].unsqueeze(4).to_broadcast([P, 4, 2, 2, LANES])
+            if k % 2:
+                nc.vector.tensor_copy(spread[:], source)
+            else:
+                nc.scalar.copy(spread[:], source)
             nc.vector.transpose(
                 wgt_sb[:, k * J // 4 : (k + 1) * J // 4], spread[:].rearrange("p c u e r -> p (c u e r)")
             )
+
+        windows = [held("window%d" % t, [P, T], F32, after="spread%d" % t) for t in range(N_TILES)]
+        for t in range(N_TILES):
+            nc.gpsimd.memset(windows[t][:].bitcast(I32), 0)
 
         def gather(dst, s, h, c0, c1):
             j0, j1 = h * HALF + c0, h * HALF + c1
@@ -149,8 +154,8 @@ def tile_list_gelu_scatb_kernel(
             return act
 
         def product(act, ub, c):
-            hid = held("hid%d" % c, [P, R], BF16)
-            nc.vector.tensor_tensor(hid[:], ub[:], act[:], MULT)
+            hid = late[0][:, 1, :].bitcast(BF16) if c == 0 else held("hid%d" % c, [P, R], BF16)[:]
+            nc.vector.tensor_tensor(hid, ub[:], act[:], MULT)
             return hid
 
         def turn(hid, index, dst):
@@ -203,7 +208,7 @@ def tile_list_gelu_scatb_kernel(
         grouped_late = [held("grouped_late%d" % k, [P, QUARTER, PACK], BF16) for k in range(2)]
         grouped1 = []
         for c in range(CHUNKS):
-            if c < 2:
+            if c == 0:
                 grouped1.append(late[0][:, c, :].bitcast(BF16).rearrange("p (j i) -> p j i", i=PACK))
             else:
                 grouped1.append(held("grouped1%d" % c, [P, CHUNK, PACK], BF16)[:])
@@ -235,8 +240,7 @@ def tile_list_gelu_scatb_kernel(
             quantize(x_codes[1, 0][:, c0:c1], x_scale[1][0][:, c0:c1], grouped1[c])
             first_layer(ga[c], 0, 1, 0, c)
             first_layer(ub[c], 1, 1, 0, c)
-        for i in (2, 3):
-            gather(late[0][:, i - 2, :], PACK + i, 1, 0, QUARTER)
+        gather(late[0][:, 0, :], last - 1, 1, 0, QUARTER)
         acts = [gate(ga[c], c) for c in range(CHUNKS)]
         hids = [product(acts[c], ub[c], c) for c in range(CHUNKS)]
         h_first = [
@@ -245,6 +249,8 @@ def tile_list_gelu_scatb_kernel(
         ]
         for c in range(CHUNKS):
             turn(hids[c], 2 * c, h_first[c // 2][:, (c % 2) * CHUNK : (c % 2 + 1) * CHUNK, :])
+            if c == 0:
+                gather(late[0][:, 1, :], last, 1, 0, QUARTER)
         for k in range(2):
             c0, c1 = k * QUARTER, (k + 1) * QUARTER
             quantize(h_codes[0][:, c0:c1], h_scale[0][:, c0:c1], h_first[k][:])

@@ -48,15 +48,14 @@ def tile_list_gelu_scatb_kernel(
         wgt_sb = held("wgt_sb", [P, J], F32)
         wgo_sb = [held("wgo_sb%d" % h, [P, HALF], F32) for h in range(2)]
         bias = held("bias", [P, N_TILES], F32)
-        w_codes = [[held("w_codes%d%d" % (m, a), [P, R], I32) for a in range(PASSES)] for m in range(2)]
-        w_scale = held("w_scale", [P, R], U8)
+        w_codes = [[held("w_codes%d%d" % (m, a), [P, R], I32)[:] for a in range(PASSES)] for m in range(2)]
+        w_scale = held("w_scale", [P, PASSES * R], U8)
         wd_codes = held("wd_codes", [P, 2 * N], U8)
         wd_scale = held("wd_scale", [P, N], U8)
         ident = held("ident", [P, P], F32)
         warm_in = held("warm_in", [P, 1], F32)
         warm_out = held("warm_out", [P, 1], F32)
-        x_codes = {}
-        x_scale = [[held("x_scale%d%d" % (a, h), [P, HALF], U8) for h in range(2)] for a in range(PASSES)]
+        x_codes, x_scale = {}, {}
         h_codes = [held("h_codes%d" % h, [P, HALF], I32) for h in range(2)]
         h_scale = [held("h_scale%d" % h, [P, HALF], U8) for h in range(2)]
 
@@ -68,8 +67,11 @@ def tile_list_gelu_scatb_kernel(
 
         def load_scales(q):
             for m, scales in enumerate((wg_scales, wu_scales)):
-                p0 = 32 * q + 8 * m
-                nc.sync.dma_start(w_scale[p0 : p0 + 8, :].bitcast(I32), scales.bitcast(I32)[:, 4 * q : 4 * q + 4, :])
+                p0 = 32 * q + 4 * m
+                nc.sync.dma_start(
+                    w_scale[p0 : p0 + 4, :].bitcast(I32).rearrange("r (a c) -> r a c", a=PASSES),
+                    scales.bitcast(I32)[:, 4 * q : 4 * q + 4, :].rearrange("a r c -> r a c"),
+                )
 
         def load_plane(s):
             a, i = divmod(s, PACK)
@@ -78,26 +80,27 @@ def tile_list_gelu_scatb_kernel(
 
         def load_words(m, a):
             words = (wg_words, wu_words)[m]
-            nc.sync.dma_start(w_codes[m][a][:], words[a].rearrange("p r i -> p (r i)").bitcast(I32))
+            nc.sync.dma_start(w_codes[m][a], words[a].rearrange("p r i -> p (r i)").bitcast(I32))
 
         last = PASSES * PACK - 1
         wgt_rows = held("wgt_rows", [P, J // LANES], F32)
         nc.sync.dma_start(wgt_rows[:], wgt[0:P:LANES, :].rearrange("g (c s) -> g c s", c=LANES))
+        load_plane(0)
         nc.sync.dma_start(picks[:], offs)
-        for s in range(last):
+        for s in range(1, last):
             load_plane(s)
             if 2 <= s < 6:
                 load_scales(s - 2)
+                nc.sync.dma_start(
+                    wd_scale[32 * (s - 2) : 32 * (s - 2) + 4, :].bitcast(I32),
+                    wd_scales[0].bitcast(I32)[4 * (s - 2) : 4 * (s - 2) + 4, :],
+                )
         load_words(0, 0)
         load_plane(last)
         load_words(1, 0)
         load_words(0, 1)
         load_words(1, 1)
         nc.sync.dma_start(wd_codes[:].bitcast(I32), wd_words[0].bitcast(I32))
-        for q in range(4):
-            nc.sync.dma_start(
-                wd_scale[32 * q : 32 * q + 4, :].bitcast(I32), wd_scales[0].bitcast(I32)[4 * q : 4 * q + 4, :]
-            )
         with nc.allow_non_contiguous_dma(reason="one bias value a partition and output tile"):
             nc.sync.dma_start(bias[:], b.rearrange("(t p) -> p t", p=P))
         nc.sync.dma_start(places[:], offs2)
@@ -124,8 +127,7 @@ def tile_list_gelu_scatb_kernel(
         for t in range(N_TILES):
             nc.gpsimd.memset(windows[t][:].bitcast(I32), 0)
 
-        def gather(dst, s, h, c0, c1):
-            j0, j1 = h * HALF + c0, h * HALF + c1
+        def gather(dst, s, j0, j1):
             nc.vector.tensor_tensor(
                 dst, planes[s][:].indirect(picks[:, j0 // LANES : j1 // LANES]), wgt_sb[:, j0:j1], MULT
             )
@@ -137,36 +139,31 @@ def tile_list_gelu_scatb_kernel(
             nc.vector.quantize_mx(out=codes.bitcast(FP8X4), scales=scales, in_=grouped.rearrange("p j i -> p (j i)"))
 
         def first_layer(acc, m, a, h, c):
-            j0 = c * CHUNK
+            piece, j0 = (2 + c // 2, c % 2 * CHUNK) if a == h == 1 else (h, c * CHUNK)
             nc.tensor.matmul_mx(
                 out=acc[:],
-                lhsT=x_codes[a, h][:, j0 : j0 + CHUNK].bitcast(FP8X4),
-                lhsT_scale=x_scale[a][h][:, j0 : j0 + CHUNK],
-                rhs=w_codes[m][a][:].bitcast(FP8X4),
-                rhs_scale=w_scale[8 * m + 4 * a :, :],
+                lhsT=x_codes[a, piece][:, j0 : j0 + CHUNK].bitcast(FP8X4),
+                lhsT_scale=x_scale[a, piece][:, j0 : j0 + CHUNK],
+                rhs=w_codes[m][a].bitcast(FP8X4),
+                rhs_scale=w_scale[4 * m :, a * R : (a + 1) * R],
                 start=(a == 0),
                 stop=(a == PASSES - 1),
             )
 
-        def gate(ga, c):
-            act = held("act%d" % c, [P, R], F32)
-            nc.scalar.activation(act[:], ga[:], GELU)
-            return act
+        def gate(act, ga):
+            nc.scalar.activation(act, ga[:], GELU)
 
-        def product(act, ub, c):
-            hid = late[0][:, 1, :].bitcast(BF16) if c == 0 else held("hid%d" % c, [P, R], BF16)[:]
-            nc.vector.tensor_tensor(hid, ub[:], act[:], MULT)
-            return hid
+        def product(hid, act, ub):
+            nc.vector.tensor_tensor(hid, ub[:], act, MULT)
 
-        def turn(hid, index, dst):
+        def transposes(hid, index, dst):
             turned = bank(index, [P, 2, CHUNK])
-            words = hid[:].bitcast(F32)
+            words = hid.bitcast(F32)
             for u in range(2):
                 nc.tensor.transpose(turned[:, u, :], words[:, u : 2 * P : 2], ident[:])
-            nc.scalar.copy(dst.bitcast(F32), turned[:].rearrange("p u j -> p j u"))
+            return dst.bitcast(F32), turned[:].rearrange("p u j -> p j u")
 
-        def second_layer(h, t, c0, c1, index, after=None, weigh=None):
-            y = held("y%d%d%d" % (h, t, c0), [P, c1 - c0], F32, after=after)
+        def down(h, t, c0, c1, index):
             acc = bank(index, [P, c1 - c0])
             nc.tensor.matmul_mx(
                 out=acc[:],
@@ -177,127 +174,222 @@ def tile_list_gelu_scatb_kernel(
                 start=True,
                 stop=True,
             )
+            return acc[:]
+
+        def target(h, t, c0, c1):
             j0, j1 = h * HALF + c0, h * HALF + c1
-            target = windows[t][:].indirect(places[:, j0 // LANES : j1 // LANES])
-            weights = wgo_sb[h][:, c0:c1]
-            if weigh == "vector":
-                nc.vector.scalar_tensor_tensor(y[:], acc[:], bias[:, t : t + 1], weights, mybir.AluOpType.add, MULT)
-                nc.vector.tensor_copy(target, y[:])
-                return
-            nc.scalar.activation(y[:], acc[:], IDENTITY, bias=bias[:, t : t + 1])
-            if weigh == "gpsimd":
-                nc.gpsimd.tensor_tensor(y[:], y[:], weights, MULT)
-                nc.vector.tensor_copy(target, y[:])
-            else:
-                nc.vector.tensor_tensor(target, y[:], weights, MULT)
+            return windows[t][:].indirect(places[:, j0 // LANES : j1 // LANES])
+
+        def biased(y, acc, t):
+            nc.scalar.activation(y, acc, IDENTITY, bias=bias[:, t : t + 1])
+
+        def weighed_on_vector(h, t, c0, c1, acc, after=None):
+            y = held("y%d%d%d" % (h, t, c0), [P, c1 - c0], F32, after=after)
+            nc.vector.scalar_tensor_tensor(
+                y[:], acc, bias[:, t : t + 1], wgo_sb[h][:, c0:c1], mybir.AluOpType.add, MULT
+            )
+            return y
+
+        def weigh_on_gpsimd(weighed, y, h, c0, c1):
+            nc.gpsimd.tensor_tensor(weighed, y, wgo_sb[h][:, c0:c1], MULT)
+
+        def place(h, t, c0, c1, weighed):
+            nc.vector.tensor_copy(target(h, t, c0, c1), weighed)
+
+        def weigh_and_place(h, t, c0, c1, y):
+            nc.vector.tensor_tensor(target(h, t, c0, c1), y, wgo_sb[h][:, c0:c1], MULT)
 
         QUARTER = HALF // 2
-        spans = [(c * CHUNK, (c + 1) * CHUNK) for c in range(CHUNKS)]
+
+        def as_grouped(rows):
+            return rows.bitcast(BF16).rearrange("p (j i) -> p j i", i=PACK)
 
         first_pass = [held("first_pass%d" % u, [P, 2, J], F32) for u in range(2)]
-        grouped0 = [held("grouped0%d" % h, [P, HALF, PACK], BF16) for h in range(2)]
+        grouped0 = held("grouped0", [P, J, PACK], BF16)
         for s in range(PACK):
-            gather(first_pass[s // 2][:, s % 2, :], s, 0, 0, J)
+            if s == 0:
+                for h in range(2):
+                    gather(first_pass[0][:, 0, h * HALF : (h + 1) * HALF], 0, h * HALF, (h + 1) * HALF)
+            else:
+                gather(first_pass[s // 2][:, s % 2, :], s, 0, J)
             if s % 2:
                 for h in range(2):
-                    interleave(grouped0[h][:, :, s - 1 : s + 1], first_pass[s // 2][:, :, h * HALF : (h + 1) * HALF])
+                    cols = slice(h * HALF, (h + 1) * HALF)
+                    interleave(grouped0[:, cols, s - 1 : s + 1], first_pass[s // 2][:, :, cols])
 
-        pair_early = held("pair_early", [P, 2, J], F32)
-        pair_last = held("pair_last", [P, 2, HALF], F32)
-        late = [held("late%d" % k, [P, 2, QUARTER], F32) for k in range(2)]
+        parts = ((0, CHUNK), (CHUNK, 2 * CHUNK), (2 * CHUNK, HALF))
+        early_head = held("early_head", [P, 2, CHUNK], F32)
+        early_rest = held("early_rest", [P, 2, J - CHUNK], F32)
+        grouped1 = [held("grouped1%d" % n, [P, c1 - c0, PACK], BF16) for n, (c0, c1) in enumerate(parts)]
         grouped_late = [held("grouped_late%d" % k, [P, QUARTER, PACK], BF16) for k in range(2)]
-        grouped1 = []
-        for c in range(CHUNKS):
-            if c == 0:
-                grouped1.append(late[0][:, c, :].bitcast(BF16).rearrange("p (j i) -> p j i", i=PACK))
-            else:
-                grouped1.append(held("grouped1%d" % c, [P, CHUNK, PACK], BF16)[:])
-        gather(pair_early[:, 0, :], PACK, 0, 0, J)
-        x_codes[0, 0] = held("x_codes00", [P, HALF], I32, after="plane4")
-        quantize(x_codes[0, 0][:], x_scale[0][0][:], grouped0[0][:])
-        for h in range(2):
-            gather(pair_early[:, 1, h * HALF : (h + 1) * HALF], PACK + 1, h, 0, HALF)
-        x_codes[0, 1] = held("x_codes01", [P, HALF], I32, after="plane5")
-        quantize(x_codes[0, 1][:], x_scale[0][1][:], grouped0[1][:])
-        for c, (c0, c1) in enumerate(spans):
-            interleave(grouped1[c][:, :, 0:2], pair_early[:, :, c0:c1])
+        gather(early_head[:, 0, :], PACK, 0, CHUNK)
+        gather(early_rest[:, 0, :], PACK, CHUNK, J)
+        gather(early_head[:, 1, :], PACK + 1, 0, CHUNK)
+        gather(early_rest[:, 1, 0 : HALF - CHUNK], PACK + 1, CHUNK, HALF)
+        gather(early_rest[:, 1, HALF - CHUNK :], PACK + 1, HALF, J)
+        interleave(grouped1[0][:, :, 0:2], early_head[:])
+        for n in (1, 2):
+            c0, c1 = parts[n]
+            interleave(grouped1[n][:, :, 0:2], early_rest[:, :, c0 - CHUNK : c1 - CHUNK])
         for k in range(2):
-            c0 = HALF + k * QUARTER
-            interleave(grouped_late[k][:, :, 0:2], pair_early[:, :, c0 : c0 + QUARTER])
-        gather(pair_last[:, 0, :], last - 1, 0, 0, HALF)
+            c0 = HALF - CHUNK + k * QUARTER
+            interleave(grouped_late[k][:, :, 0:2], early_rest[:, :, c0 : c0 + QUARTER])
+        codes0 = held("x_codes0", [P, J], I32)
+        scale0 = held("x_scale0", [P, J], U8, after="early_head")
+        for h in range(2):
+            cols = slice(h * HALF, (h + 1) * HALF)
+            x_codes[0, h], x_scale[0, h] = codes0[:, cols], scale0[:, cols]
+            quantize(x_codes[0, h], x_scale[0, h], grouped0[:, cols, :])
+        x_codes[1, 0] = held("x_codes10", [P, HALF], I32)[:]
+        x_scale[1, 0] = held("x_scale10", [P, HALF], U8)[:]
+        last_two = held("last_two", [P, CHUNK + 2 * HALF], F32)
+        pair_last = last_two[:, CHUNK:].rearrange("p (i j) -> p i j", i=2)
+        gather(pair_last[:, 0, :], last - 1, 0, HALF)
         ga = [bank(2 * c, [P, R]) for c in range(CHUNKS)]
         ub = [bank(2 * c + 1, [P, R]) for c in range(CHUNKS)]
         for c in range(CHUNKS):
             first_layer(ga[c], 0, 0, 0, c)
-        for c in range(CHUNKS):
-            first_layer(ub[c], 1, 0, 0, c)
 
-        x_codes[1, 0] = held("x_codes10", [P, HALF], I32)
-        for c, (c0, c1) in enumerate(spans):
-            gather(pair_last[:, 1, c0:c1], last, 0, c0, c1)
-            interleave(grouped1[c][:, :, 2:4], pair_last[:, :, c0:c1])
-        for c, (c0, c1) in enumerate(spans):
-            quantize(x_codes[1, 0][:, c0:c1], x_scale[1][0][:, c0:c1], grouped1[c])
+        for n, (c0, c1) in enumerate(parts):
+            gather(pair_last[:, 1, c0:c1], last, c0, c1)
+        acts = [held("act%d" % c, [P, R], F32)[:] for c in range(CHUNKS)]
+        hids = [
+            last_two[:, 0:QUARTER].bitcast(BF16),
+            held("hid1", [P, R], BF16)[:],
+            pair_last[:, 1, QUARTER:].bitcast(BF16),
+            held("hid3", [P, R], BF16)[:],
+        ]
+        h_first = [held("h_first%d" % k, [P, QUARTER, PACK], BF16) for k in range(2)]
+
+        def x_part(n):
+            c0, c1 = parts[n]
+            interleave(grouped1[n][:, :, 2:4], pair_last[:, :, c0:c1])
+            quantize(x_codes[1, 0][:, c0:c1], x_scale[1, 0][:, c0:c1], grouped1[n][:])
+
+        def late_gather(i, c0, c1):
+            gather(pair_last[:, i, c0:c1], last - 1 + i, HALF + c0, HALF + c1)
+
+        def late_interleave(k):
+            interleave(grouped_late[k][:, :, 2:4], pair_last[:, :, k * QUARTER : (k + 1) * QUARTER])
+
+        def first_transposes(c, index):
+            return transposes(hids[c], index, h_first[c // 2][:, (c % 2) * CHUNK : (c % 2 + 1) * CHUNK, :])
+
+        def first_turn(c, index):
+            nc.scalar.copy(*first_transposes(c, index))
+
+        def late_quantize(k, after=None):
+            x_codes[1, 2 + k] = held("x_codes_late%d" % k, [P, QUARTER], I32, after=after)[:]
+            x_scale[1, 2 + k] = held("x_scale_late%d" % k, [P, QUARTER], U8)[:]
+            quantize(x_codes[1, 2 + k], x_scale[1, 2 + k], grouped_late[k][:])
+
+        first_layer(ub[0], 1, 0, 0, 0)
+        first_layer(ub[1], 1, 0, 0, 1)
+        x_part(0)
+        first_layer(ga[0], 0, 1, 0, 0)
+        first_layer(ub[2], 1, 0, 0, 2)
+        late_gather(1, 0, CHUNK)
+        x_part(1)
+        first_layer(ga[1], 0, 1, 0, 1)
+        first_layer(ub[0], 1, 1, 0, 0)
+        first_layer(ub[1], 1, 1, 0, 1)
+        first_layer(ub[3], 1, 0, 0, 3)
+        late_gather(0, CHUNK, QUARTER)
+        late_gather(1, CHUNK, QUARTER)
+        x_part(2)
+        late_gather(0, QUARTER, HALF)
+        for c in (2, 3):
             first_layer(ga[c], 0, 1, 0, c)
             first_layer(ub[c], 1, 1, 0, c)
-        gather(late[0][:, 0, :], last - 1, 1, 0, QUARTER)
-        acts = [gate(ga[c], c) for c in range(CHUNKS)]
-        hids = [product(acts[c], ub[c], c) for c in range(CHUNKS)]
-        h_first = [
-            late[1][:].rearrange("p i j -> p (i j)").bitcast(BF16).rearrange("p (j i) -> p j i", i=PACK),
-            held("h_first1", [P, QUARTER, PACK], BF16)[:],
-        ]
         for c in range(CHUNKS):
-            turn(hids[c], 2 * c, h_first[c // 2][:, (c % 2) * CHUNK : (c % 2 + 1) * CHUNK, :])
-            if c == 0:
-                gather(late[0][:, 1, :], last, 1, 0, QUARTER)
-        for k in range(2):
-            c0, c1 = k * QUARTER, (k + 1) * QUARTER
-            quantize(h_codes[0][:, c0:c1], h_scale[0][:, c0:c1], h_first[k][:])
-            if k == 0:
-                for i in (2, 3):
-                    gather(late[1][:, i - 2, :], PACK + i, 1, QUARTER, HALF)
-        second_layer(0, 0, 0, QUARTER, 1, weigh="vector")
-        second_layer(0, 1, 0, QUARTER, 3, weigh="vector")
+            gate(acts[c], ga[c])
+        product(hids[0], acts[0], ub[0])
+        product(hids[1], acts[1], ub[1])
+        first_turn(0, 0)
+        first_turn(1, 2)
+        product(hids[2], acts[2], ub[2])
+        late_gather(0, 0, CHUNK)
+        product(hids[3], acts[3], ub[3])
+        late_interleave(0)
+        quantize(h_codes[0][:, 0:QUARTER], h_scale[0][:, 0:QUARTER], h_first[0][:])
+        hand_over = first_transposes(2, 0)
+        late_gather(1, QUARTER, HALF)
+        nc.vector.tensor_copy(*hand_over)
+        first_turn(3, 2)
+        accs = [down(0, t, 0, QUARTER, index) for t, index in enumerate((4, 6))]
+        late_quantize(0)
+        first0 = weighed_on_vector(0, 0, 0, QUARTER, accs[0])
+        quantize(h_codes[0][:, QUARTER:HALF], h_scale[0][:, QUARTER:HALF], h_first[1][:])
+        first1 = weighed_on_vector(0, 1, 0, QUARTER, accs[1])
+        late_interleave(1)
+        late_quantize(1)
+        place(0, 0, 0, QUARTER, first0[:])
+        place(0, 1, 0, QUARTER, first1[:])
 
-        x_codes[1, 1] = held("x_codes11", [P, HALF], I32)
+        banks = ((4, 6), (0, 2), (5, 7), (1, 4))
+        ga, ub = {}, {}
 
-        def late_pass(k):
-            grouped = grouped_late[k]
-            for c0 in range(0, QUARTER, CHUNK):
-                interleave(grouped[:, c0 : c0 + CHUNK, 2:4], late[k][:, :, c0 : c0 + CHUNK])
-            c0, c1 = k * QUARTER, (k + 1) * QUARTER
-            quantize(x_codes[1, 1][:, c0:c1], x_scale[1][1][:, c0:c1], grouped[:])
-
-        late_pass(0)
-        second_layer(0, 2, 0, HALF, 5, weigh="gpsimd")
-        late_pass(1)
-        second_layer(0, 0, QUARTER, HALF, 7, weigh="gpsimd")
-        second_layer(0, 1, QUARTER, HALF, 1, weigh="gpsimd")
-        banks = ((0, 2), (4, 6), (1, 3), (7, 5))
-        ga = [bank(g_bank, [P, R]) for g_bank, u_bank in banks]
-        ub = [bank(u_bank, [P, R]) for g_bank, u_bank in banks]
-        for a in range(PASSES):
-            for c in range(CHUNKS):
+        def second_first_layer(c):
+            ga[c], ub[c] = bank(banks[c][0], [P, R]), bank(banks[c][1], [P, R])
+            for a in range(PASSES):
                 first_layer(ga[c], 0, a, 1, c)
                 first_layer(ub[c], 1, a, 1, c)
-        h_second = [held("h_second%d" % k, [P, QUARTER, PACK], BF16) for k in range(2)]
-        hids = []
+
+        act_pairs = [held("act_pair%d" % k, [P, 2, R], F32, after="plane%d" % k) for k in range(2)]
+        up_flat = [held("up_pair%d" % k, [P, 2 * R + HALF - CHUNK], F32, after="plane%d" % (2 + k)) for k in range(2)]
+        up_pairs = [flat[:, 0 : 2 * R].rearrange("p (k r) -> p k r", k=2) for flat in up_flat]
+
+        def leave_banks(c):
+            gate(act_pairs[c // 2][:, c % 2, :], ga[c])
+            nc.scalar.copy(up_pairs[c // 2][:, c % 2, :], ub[c][:])
+
+        y2 = held("y02", [P, HALF], F32)
+        biased(y2[:], down(0, 2, 0, HALF, 5), 2)
+        weighed2 = held("weighed02", [P, HALF], F32, after="grouped_late1")
+        weigh_on_gpsimd(weighed2[:], y2[:], 0, 0, HALF)
+        place(0, 2, 0, HALF, weighed2[:])
+        accs = [down(0, t, QUARTER, HALF, index) for t, index in enumerate((7, 1))]
+        acc3 = down(0, 3, 0, HALF, 3)
+        ys = held("y0b", [P, 2, QUARTER], F32)
+        weighed = held("weighed0b", [P, 2, QUARTER], F32)
+        for t in range(2):
+            biased(ys[:, t, :], accs[t], t)
+        both = wgo_sb[0][:, QUARTER:HALF].unsqueeze(1).to_broadcast([P, 2, QUARTER])
+        nc.gpsimd.tensor_tensor(weighed[:], ys[:], both, MULT)
+        for t in range(2):
+            place(0, t, QUARTER, HALF, weighed[:, t, :])
         for c in range(CHUNKS):
-            act = gate(ga[c], CHUNKS + c)
-            up = held("up%d" % c, [P, R], F32, after="plane%d" % c)
-            nc.scalar.copy(up[:], ub[c][:])
-            hid = held("hid%d" % (CHUNKS + c), [P, R], BF16)
-            nc.gpsimd.tensor_tensor(hid[:], up[:], act[:], MULT)
-            hids.append(hid)
+            second_first_layer(c)
+            leave_banks(c)
+        hid_second = held("hid_second", [P, CHUNKS, R], BF16, after="y02")
+        hids = [hid_second[:, c, :] for c in range(CHUNKS)]
+        h_second = [held("h_second%d" % k, [P, QUARTER, PACK], BF16) for k in range(2)]
+
+        def second_turn(c, index):
+            nc.scalar.copy(*transposes(hids[c], index, h_second[c // 2][:, (c % 2) * CHUNK : (c % 2 + 1) * CHUNK, :]))
+
         for k in range(2):
-            for c in (2 * k, 2 * k + 1):
-                turn(hids[c], banks[c][1], h_second[k][:, (c % 2) * CHUNK : (c % 2 + 1) * CHUNK, :])
-            c0, c1 = k * QUARTER, (k + 1) * QUARTER
-            quantize(h_codes[1][:, c0:c1], h_scale[1][:, c0:c1], h_second[k][:])
-            if k == 0:
-                second_layer(0, 3, 0, HALF, 0, after="hid4", weigh="gpsimd")
-        second_layer(1, 0, 0, QUARTER, 4, after="hid7")
-        for t, c0, index in ((1, 0, 1), (0, QUARTER, 7), (2, 0, 2), (3, 0, 6)):
-            second_layer(1, t, c0, HALF, index)
+            nc.gpsimd.tensor_tensor(hid_second[:, 2 * k : 2 * k + 2, :], up_pairs[k], act_pairs[k][:], MULT)
+        second_turn(0, 6)
+        second_turn(1, 0)
+        quantize(h_codes[1][:, 0:QUARTER], h_scale[1][:, 0:QUARTER], h_second[0][:])
+        second_turn(2, 2)
+        y3 = up_flat[1][:, 2 * R - CHUNK :]
+        biased(y3[:, CHUNK:], acc3[:, CHUNK:], 3)
+        biased(y3[:, 0:CHUNK], acc3[:, 0:CHUNK], 3)
+        weigh_and_place(0, 3, 0, HALF, y3)
+        second_turn(3, 5)
+        quantize(h_codes[1][:, QUARTER:HALF], h_scale[1][:, QUARTER:HALF], h_second[1][:])
+        y0 = held("y10a", [P, QUARTER], F32)
+        biased(y0[:], down(1, 0, 0, QUARTER, 5), 0)
+        weigh_and_place(1, 0, 0, QUARTER, y0[:])
+        y1 = held("y11", [P, HALF], F32)
+        biased(y1[:, 0:QUARTER], down(1, 1, 0, QUARTER, 2), 1)
+        biased(y1[:, QUARTER:HALF], down(1, 1, QUARTER, HALF, 0), 1)
+        weigh_and_place(1, 1, 0, HALF, y1[:])
+        nc.sync.dma_start(out[P : 2 * P, :], windows[1][:])
+        for t, c0, index in ((0, QUARTER, 7), (2, 0, 1), (3, 0, 6)):
+            y = held("y1%d%d" % (t, c0), [P, HALF - c0], F32)
+            biased(y[:], down(1, t, c0, HALF, index), t)
+            weigh_and_place(1, t, c0, HALF, y[:])
             nc.sync.dma_start(out[P * t : P * (t + 1), :], windows[t][:])

@@ -49,7 +49,7 @@ def tile_list_gelu_scatb_kernel(
         wgo_sb = [held("wgo_sb%d" % h, [P, HALF], F32) for h in range(2)]
         bias = held("bias", [P, N_TILES], F32)
         w_codes = [[held("w_codes%d%d" % (m, a), [P, R], I32)[:] for a in range(PASSES)] for m in range(2)]
-        w_scale = held("w_scale", [P, PASSES * R], U8)
+        w_scale = [held("w_scale%d" % m, [P, PASSES * R], U8) for m in range(2)]
         wd_codes = held("wd_codes", [P, 2 * N], U8)
         wd_scale = held("wd_scale", [P, N], U8)
         ident = held("ident", [P, P], F32)
@@ -61,17 +61,22 @@ def tile_list_gelu_scatb_kernel(
 
         nc.gpsimd.memset(warm_in[:], 0.0)
         nc.scalar.activation(warm_out[:], warm_in[:], GELU)
-        nc.gpsimd.memset(w_scale[:].bitcast(I32), 0)
+        for m in range(2):
+            nc.gpsimd.memset(w_scale[m][:].bitcast(I32), 0)
         nc.gpsimd.memset(wd_scale[:].bitcast(I32), 0)
         make_identity(nc, ident[:])
 
-        def load_scales(q):
-            for m, scales in enumerate((wg_scales, wu_scales)):
-                p0 = 32 * q + 4 * m
-                nc.sync.dma_start(
-                    w_scale[p0 : p0 + 4, :].bitcast(I32).rearrange("r (a c) -> r a c", a=PASSES),
-                    scales.bitcast(I32)[:, 4 * q : 4 * q + 4, :].rearrange("a r c -> r a c"),
-                )
+        def load_scales(m, q):
+            scales = (wg_scales, wu_scales)[m]
+            nc.sync.dma_start(
+                w_scale[m][32 * q : 32 * q + 4, :].bitcast(I32).rearrange("r (a c) -> r a c", a=PASSES),
+                scales.bitcast(I32)[:, 4 * q : 4 * q + 4, :].rearrange("a r c -> r a c"),
+            )
+
+        def load_down_scales(q):
+            nc.sync.dma_start(
+                wd_scale[32 * q : 32 * q + 4, :].bitcast(I32), wd_scales[0].bitcast(I32)[4 * q : 4 * q + 4, :]
+            )
 
         def load_plane(s):
             a, i = divmod(s, PACK)
@@ -89,23 +94,27 @@ def tile_list_gelu_scatb_kernel(
         nc.sync.dma_start(picks[:], offs)
         for s in range(1, last):
             load_plane(s)
-            if 2 <= s < 6:
-                load_scales(s - 2)
-                nc.sync.dma_start(
-                    wd_scale[32 * (s - 2) : 32 * (s - 2) + 4, :].bitcast(I32),
-                    wd_scales[0].bitcast(I32)[4 * (s - 2) : 4 * (s - 2) + 4, :],
-                )
+            if s <= PACK:
+                load_scales(0, s - 1)
+            if s == PACK + 1:
+                load_down_scales(3)
         load_words(0, 0)
         load_plane(last)
-        load_words(1, 0)
-        load_words(0, 1)
-        load_words(1, 1)
-        nc.sync.dma_start(wd_codes[:].bitcast(I32), wd_words[0].bitcast(I32))
-        with nc.allow_non_contiguous_dma(reason="one bias value a partition and output tile"):
-            nc.sync.dma_start(bias[:], b.rearrange("(t p) -> p t", p=P))
-        nc.sync.dma_start(places[:], offs2)
-        for h in range(2):
-            nc.sync.dma_start(wgo_sb[h][:], wgo[:, h * HALF : (h + 1) * HALF])
+
+        def load_the_rest():
+            for q in range(4):
+                load_scales(1, q)
+            load_words(1, 0)
+            load_words(0, 1)
+            load_words(1, 1)
+            nc.sync.dma_start(wd_codes[:].bitcast(I32), wd_words[0].bitcast(I32))
+            for q in range(3):
+                load_down_scales(q)
+            with nc.allow_non_contiguous_dma(reason="one bias value a partition and output tile"):
+                nc.sync.dma_start(bias[:], b.rearrange("(t p) -> p t", p=P))
+            nc.sync.dma_start(places[:], offs2)
+            for h in range(2):
+                nc.sync.dma_start(wgo_sb[h][:], wgo[:, h * HALF : (h + 1) * HALF])
 
         SQUARE = 32
         wgt_turned = held("wgt_turned", [P, 2, SQUARE], F32)
@@ -145,7 +154,7 @@ def tile_list_gelu_scatb_kernel(
                 lhsT=x_codes[a, piece][:, j0 : j0 + CHUNK].bitcast(FP8X4),
                 lhsT_scale=x_scale[a, piece][:, j0 : j0 + CHUNK],
                 rhs=w_codes[m][a].bitcast(FP8X4),
-                rhs_scale=w_scale[4 * m :, a * R : (a + 1) * R],
+                rhs_scale=w_scale[m][:, a * R : (a + 1) * R],
                 start=(a == 0),
                 stop=(a == PASSES - 1),
             )
@@ -218,28 +227,27 @@ def tile_list_gelu_scatb_kernel(
                     interleave(grouped0[:, cols, s - 1 : s + 1], first_pass[s // 2][:, :, cols])
 
         parts = ((0, CHUNK), (CHUNK, 2 * CHUNK), (2 * CHUNK, HALF))
-        early_head = held("early_head", [P, 2, CHUNK], F32)
-        early_rest = held("early_rest", [P, 2, J - CHUNK], F32)
+        early = held("early", [P, 2, J], F32)
         grouped1 = [held("grouped1%d" % n, [P, c1 - c0, PACK], BF16) for n, (c0, c1) in enumerate(parts)]
         grouped_late = [held("grouped_late%d" % k, [P, QUARTER, PACK], BF16) for k in range(2)]
-        gather(early_head[:, 0, :], PACK, 0, CHUNK)
-        gather(early_rest[:, 0, :], PACK, CHUNK, J)
-        gather(early_head[:, 1, :], PACK + 1, 0, CHUNK)
-        gather(early_rest[:, 1, 0 : HALF - CHUNK], PACK + 1, CHUNK, HALF)
-        gather(early_rest[:, 1, HALF - CHUNK :], PACK + 1, HALF, J)
-        interleave(grouped1[0][:, :, 0:2], early_head[:])
-        for n in (1, 2):
-            c0, c1 = parts[n]
-            interleave(grouped1[n][:, :, 0:2], early_rest[:, :, c0 - CHUNK : c1 - CHUNK])
-        for k in range(2):
-            c0 = HALF - CHUNK + k * QUARTER
-            interleave(grouped_late[k][:, :, 0:2], early_rest[:, :, c0 : c0 + QUARTER])
         codes0 = held("x_codes0", [P, J], I32)
-        scale0 = held("x_scale0", [P, J], U8, after="early_head")
-        for h in range(2):
+
+        def first_pass_quantize(h):
             cols = slice(h * HALF, (h + 1) * HALF)
-            x_codes[0, h], x_scale[0, h] = codes0[:, cols], scale0[:, cols]
+            x_codes[0, h], x_scale[0, h] = codes0[:, cols], (w_scale[0], wd_scale)[h][4:, 0:HALF]
             quantize(x_codes[0, h], x_scale[0, h], grouped0[:, cols, :])
+
+        gather(early[:, 0, :], PACK, 0, J)
+        first_pass_quantize(0)
+        for h in range(2):
+            gather(early[:, 1, h * HALF : (h + 1) * HALF], PACK + 1, h * HALF, (h + 1) * HALF)
+        first_pass_quantize(1)
+        load_the_rest()
+        for n, (c0, c1) in enumerate(parts):
+            interleave(grouped1[n][:, :, 0:2], early[:, :, c0:c1])
+        for k in range(2):
+            c0 = HALF + k * QUARTER
+            interleave(grouped_late[k][:, :, 0:2], early[:, :, c0 : c0 + QUARTER])
         x_codes[1, 0] = held("x_codes10", [P, HALF], I32)[:]
         x_scale[1, 0] = held("x_scale10", [P, HALF], U8)[:]
         last_two = held("last_two", [P, CHUNK + 2 * HALF], F32)
@@ -320,13 +328,16 @@ def tile_list_gelu_scatb_kernel(
         late_quantize(0)
         first0 = weighed_on_vector(0, 0, 0, QUARTER, accs[0])
         quantize(h_codes[0][:, QUARTER:HALF], h_scale[0][:, QUARTER:HALF], h_first[1][:])
-        first1 = weighed_on_vector(0, 1, 0, QUARTER, accs[1])
         late_interleave(1)
-        late_quantize(1)
+        y1 = held("y01a", [P, QUARTER], F32)
+        biased(y1[:], accs[1], 1)
+        first1 = held("weighed01a", [P, QUARTER], F32, after="h_first1")
+        weigh_on_gpsimd(first1[:], y1[:], 0, 0, QUARTER)
         place(0, 0, 0, QUARTER, first0[:])
+        late_quantize(1)
         place(0, 1, 0, QUARTER, first1[:])
 
-        banks = ((4, 6), (0, 2), (5, 7), (1, 4))
+        banks = ((0, 2), (4, 6), (5, 7), (1, 3))
         ga, ub = {}, {}
 
         def second_first_layer(c):
@@ -349,7 +360,6 @@ def tile_list_gelu_scatb_kernel(
         weigh_on_gpsimd(weighed2[:], y2[:], 0, 0, HALF)
         place(0, 2, 0, HALF, weighed2[:])
         accs = [down(0, t, QUARTER, HALF, index) for t, index in enumerate((7, 1))]
-        acc3 = down(0, 3, 0, HALF, 3)
         ys = held("y0b", [P, 2, QUARTER], F32)
         weighed = held("weighed0b", [P, 2, QUARTER], F32)
         for t in range(2):
@@ -361,6 +371,7 @@ def tile_list_gelu_scatb_kernel(
         for c in range(CHUNKS):
             second_first_layer(c)
             leave_banks(c)
+        acc3 = down(0, 3, 0, HALF, 5)
         hid_second = held("hid_second", [P, CHUNKS, R], BF16, after="y02")
         hids = [hid_second[:, c, :] for c in range(CHUNKS)]
         h_second = [held("h_second%d" % k, [P, QUARTER, PACK], BF16) for k in range(2)]
@@ -370,25 +381,25 @@ def tile_list_gelu_scatb_kernel(
 
         for k in range(2):
             nc.gpsimd.tensor_tensor(hid_second[:, 2 * k : 2 * k + 2, :], up_pairs[k], act_pairs[k][:], MULT)
-        second_turn(0, 6)
-        second_turn(1, 0)
+        second_turn(0, 2)
+        second_turn(1, 4)
         quantize(h_codes[1][:, 0:QUARTER], h_scale[1][:, 0:QUARTER], h_second[0][:])
-        second_turn(2, 2)
+        second_turn(2, 6)
         y3 = up_flat[1][:, 2 * R - CHUNK :]
         biased(y3[:, CHUNK:], acc3[:, CHUNK:], 3)
         biased(y3[:, 0:CHUNK], acc3[:, 0:CHUNK], 3)
         weigh_and_place(0, 3, 0, HALF, y3)
-        second_turn(3, 5)
+        second_turn(3, 7)
         quantize(h_codes[1][:, QUARTER:HALF], h_scale[1][:, QUARTER:HALF], h_second[1][:])
         y0 = held("y10a", [P, QUARTER], F32)
-        biased(y0[:], down(1, 0, 0, QUARTER, 5), 0)
+        biased(y0[:], down(1, 0, 0, QUARTER, 7), 0)
         weigh_and_place(1, 0, 0, QUARTER, y0[:])
         y1 = held("y11", [P, HALF], F32)
-        biased(y1[:, 0:QUARTER], down(1, 1, 0, QUARTER, 2), 1)
-        biased(y1[:, QUARTER:HALF], down(1, 1, QUARTER, HALF, 0), 1)
+        biased(y1[:, 0:QUARTER], down(1, 1, 0, QUARTER, 6), 1)
+        biased(y1[:, QUARTER:HALF], down(1, 1, QUARTER, HALF, 4), 1)
         weigh_and_place(1, 1, 0, HALF, y1[:])
         nc.sync.dma_start(out[P : 2 * P, :], windows[1][:])
-        for t, c0, index in ((0, QUARTER, 7), (2, 0, 1), (3, 0, 6)):
+        for t, c0, index in ((0, QUARTER, 0), (2, 0, 1), (3, 0, 2)):
             y = held("y1%d%d" % (t, c0), [P, HALF - c0], F32)
             biased(y[:], down(1, t, c0, HALF, index), t)
             weigh_and_place(1, t, c0, HALF, y[:])

@@ -94,10 +94,12 @@ def tile_list_gelu_scatb_kernel(
         nc.sync.dma_start(picks[:], offs)
         for s in range(1, last):
             load_plane(s)
-            if s <= PACK:
+            if s < PACK:
                 load_scales(0, s - 1)
+                load_down_scales(s - 1)
             if s == PACK + 1:
                 load_down_scales(3)
+                load_scales(0, 3)
         load_words(0, 0)
         load_plane(last)
 
@@ -108,8 +110,6 @@ def tile_list_gelu_scatb_kernel(
             load_words(0, 1)
             load_words(1, 1)
             nc.sync.dma_start(wd_codes[:].bitcast(I32), wd_words[0].bitcast(I32))
-            for q in range(3):
-                load_down_scales(q)
             with nc.allow_non_contiguous_dma(reason="one bias value a partition and output tile"):
                 nc.sync.dma_start(bias[:], b.rearrange("(t p) -> p t", p=P))
             nc.sync.dma_start(places[:], offs2)
@@ -234,14 +234,13 @@ def tile_list_gelu_scatb_kernel(
 
         def first_pass_quantize(h):
             cols = slice(h * HALF, (h + 1) * HALF)
-            x_codes[0, h], x_scale[0, h] = codes0[:, cols], (w_scale[0], wd_scale)[h][4:, 0:HALF]
+            x_codes[0, h], x_scale[0, h] = codes0[:, cols], (wd_scale[4:, :], w_scale[0][4:, R:])[h]
             quantize(x_codes[0, h], x_scale[0, h], grouped0[:, cols, :])
 
         gather(early[:, 0, :], PACK, 0, J)
-        first_pass_quantize(0)
         for h in range(2):
             gather(early[:, 1, h * HALF : (h + 1) * HALF], PACK + 1, h * HALF, (h + 1) * HALF)
-        first_pass_quantize(1)
+            first_pass_quantize(h)
         load_the_rest()
         for n, (c0, c1) in enumerate(parts):
             interleave(grouped1[n][:, :, 0:2], early[:, :, c0:c1])
@@ -250,8 +249,8 @@ def tile_list_gelu_scatb_kernel(
             interleave(grouped_late[k][:, :, 0:2], early[:, :, c0 : c0 + QUARTER])
         x_codes[1, 0] = held("x_codes10", [P, HALF], I32)[:]
         x_scale[1, 0] = held("x_scale10", [P, HALF], U8)[:]
-        last_two = held("last_two", [P, CHUNK + 2 * HALF], F32)
-        pair_last = last_two[:, CHUNK:].rearrange("p (i j) -> p i j", i=2)
+        last_two = held("last_two", [P, 2 * HALF + QUARTER], F32)
+        pair_last = last_two[:, 0 : 2 * HALF].rearrange("p (i j) -> p i j", i=2)
         gather(pair_last[:, 0, :], last - 1, 0, HALF)
         ga = [bank(2 * c, [P, R]) for c in range(CHUNKS)]
         ub = [bank(2 * c + 1, [P, R]) for c in range(CHUNKS)]
@@ -262,9 +261,9 @@ def tile_list_gelu_scatb_kernel(
             gather(pair_last[:, 1, c0:c1], last, c0, c1)
         acts = [held("act%d" % c, [P, R], F32)[:] for c in range(CHUNKS)]
         hids = [
-            last_two[:, 0:QUARTER].bitcast(BF16),
+            last_two[:, CHUNK : CHUNK + QUARTER].bitcast(BF16),
             held("hid1", [P, R], BF16)[:],
-            pair_last[:, 1, QUARTER:].bitcast(BF16),
+            last_two[:, 2 * HALF :].bitcast(BF16),
             held("hid3", [P, R], BF16)[:],
         ]
         h_first = [held("h_first%d" % k, [P, QUARTER, PACK], BF16) for k in range(2)]
@@ -274,11 +273,14 @@ def tile_list_gelu_scatb_kernel(
             interleave(grouped1[n][:, :, 2:4], pair_last[:, :, c0:c1])
             quantize(x_codes[1, 0][:, c0:c1], x_scale[1, 0][:, c0:c1], grouped1[n][:])
 
-        def late_gather(i, c0, c1):
-            gather(pair_last[:, i, c0:c1], last - 1 + i, HALF + c0, HALF + c1)
+        late = [pair_last[:, :, 0:QUARTER], last_two[:, HALF + QUARTER :].rearrange("p (i j) -> p i j", i=2)]
+
+        def late_gather(k, i, c0, c1):
+            j0 = HALF + k * QUARTER
+            gather(late[k][:, i, c0:c1], last - 1 + i, j0 + c0, j0 + c1)
 
         def late_interleave(k):
-            interleave(grouped_late[k][:, :, 2:4], pair_last[:, :, k * QUARTER : (k + 1) * QUARTER])
+            interleave(grouped_late[k][:, :, 2:4], late[k])
 
         def first_transposes(c, index):
             return transposes(hids[c], index, h_first[c // 2][:, (c % 2) * CHUNK : (c % 2 + 1) * CHUNK, :])
@@ -296,16 +298,15 @@ def tile_list_gelu_scatb_kernel(
         x_part(0)
         first_layer(ga[0], 0, 1, 0, 0)
         first_layer(ub[2], 1, 0, 0, 2)
-        late_gather(1, 0, CHUNK)
+        late_gather(0, 0, 0, CHUNK)
         x_part(1)
         first_layer(ga[1], 0, 1, 0, 1)
         first_layer(ub[0], 1, 1, 0, 0)
         first_layer(ub[1], 1, 1, 0, 1)
         first_layer(ub[3], 1, 0, 0, 3)
-        late_gather(0, CHUNK, QUARTER)
-        late_gather(1, CHUNK, QUARTER)
+        late_gather(0, 1, 0, QUARTER)
         x_part(2)
-        late_gather(0, QUARTER, HALF)
+        late_gather(1, 0, 0, QUARTER)
         for c in (2, 3):
             first_layer(ga[c], 0, 1, 0, c)
             first_layer(ub[c], 1, 1, 0, c)
@@ -316,12 +317,12 @@ def tile_list_gelu_scatb_kernel(
         first_turn(0, 0)
         first_turn(1, 2)
         product(hids[2], acts[2], ub[2])
-        late_gather(0, 0, CHUNK)
+        late_gather(0, 0, CHUNK, QUARTER)
         product(hids[3], acts[3], ub[3])
         late_interleave(0)
         quantize(h_codes[0][:, 0:QUARTER], h_scale[0][:, 0:QUARTER], h_first[0][:])
         hand_over = first_transposes(2, 0)
-        late_gather(1, QUARTER, HALF)
+        late_gather(1, 1, 0, QUARTER)
         nc.vector.tensor_copy(*hand_over)
         first_turn(3, 2)
         accs = [down(0, t, 0, QUARTER, index) for t, index in enumerate((4, 6))]
@@ -403,4 +404,7 @@ def tile_list_gelu_scatb_kernel(
             y = held("y1%d%d" % (t, c0), [P, HALF - c0], F32)
             biased(y[:], down(1, t, c0, HALF, index), t)
             weigh_and_place(1, t, c0, HALF, y[:])
-            nc.sync.dma_start(out[P * t : P * (t + 1), :], windows[t][:])
+            if t < N_TILES - 1:
+                nc.sync.dma_start(out[P * t : P * (t + 1), :], windows[t][:])
+        for queue, c0 in ((nc.sync, 0), (nc.scalar, T // 2)):
+            queue.dma_start(out[N - P : N, c0 : c0 + T // 2], windows[N_TILES - 1][:, c0 : c0 + T // 2])

@@ -25,7 +25,6 @@ CHUNK = 128
 CHUNKS = HALF // CHUNK
 N_TILES = N // P
 LANES = 16
-SPLIT = 128
 
 
 def tile_list_gelu_scatb_kernel(
@@ -216,11 +215,7 @@ def tile_list_gelu_scatb_kernel(
         first_pass = [held("first_pass%d" % u, [P, 2, J], F32) for u in range(2)]
         grouped0 = held("grouped0", [P, J, PACK], BF16)
         for s in range(PACK):
-            if s == 0:
-                for h in range(2):
-                    gather(first_pass[0][:, 0, h * HALF : (h + 1) * HALF], 0, h * HALF, (h + 1) * HALF)
-            else:
-                gather(first_pass[s // 2][:, s % 2, :], s, 0, J)
+            gather(first_pass[s // 2][:, s % 2, :], s, 0, J)
             if s % 2:
                 for h in range(2):
                     cols = slice(h * HALF, (h + 1) * HALF)

from contextlib import ExitStack

import concourse.mybir as mybir
from concourse.masks import make_identity

K, R, N, T, J = 1024, 512, 512, 2048, 1024
FLOPS = 2 * J * (2 * K * R + R * N)

F32 = mybir.dt.float32
BF16 = mybir.dt.bfloat16
I32 = mybir.dt.int32
U16 = mybir.dt.uint16
U8 = mybir.dt.uint8
FP8X4 = mybir.dt.float8_e4m3fn_x4
FP4X4 = mybir.dt.float4_e2m1fn_x4
MULT = mybir.AluOpType.mult
GELU = mybir.ActivationFunctionType.Gelu_apprx_tanh
IDENTITY = mybir.ActivationFunctionType.Identity

P = 128
PACK = 4
PASSES = K // (P * PACK)
HALF = J // 2
CHUNK = 128
CHUNKS = HALF // CHUNK
N_TILES = N // P
LANES = 16


def tile_list_gelu_scatb_kernel(
    tc, xT, wgt, wg_words, wg_scales, wu_words, wu_scales, wd_words, wd_scales, b, wgo, offs, offs2, out
):
    nc = tc.nc
    with ExitStack() as ctx:
        keep = ctx.enter_context(tc.tile_pool(name="keep", bufs=1))
        psum = ctx.enter_context(tc.psum_pool(name="psum", bufs=1))

        def held(name, shape, dtype, bufs=1, after=None):
            return keep.tile(shape, dtype, name=name, tag=after or name, bufs=bufs, align_bytes=64)

        def bank(index, shape):
            return psum.tile(shape, F32, name="bank%d" % index, tag="bank%d" % index)

        picks = held("picks", [P, J // LANES], U16)
        places = held("places", [P, J // LANES], U16)
        planes = [held("plane%d" % s, [P, T], F32) for s in range(PASSES * PACK)]
        wgt_sb = held("wgt_sb", [P, J], F32)
        wgo_sb = [held("wgo_sb%d" % h, [P, HALF], F32) for h in range(2)]
        bias = held("bias", [P, N_TILES], F32)
        w_codes = [[held("w_codes%d%d" % (m, a), [P, R], I32)[:] for a in range(PASSES)] for m in range(2)]
        w_scale = [held("w_scale%d" % m, [P, PASSES * R], U8) for m in range(2)]
        wd_codes = held("wd_codes", [P, 2 * N], U8)
        wd_scale = held("wd_scale", [P, N], U8)
        ident = held("ident", [P, P], F32)
        warm_in = held("warm_in", [P, 1], F32)
        warm_out = held("warm_out", [P, 1], F32)
        x_codes, x_scale = {}, {}
        h_codes = [held("h_codes%d" % h, [P, HALF], I32) for h in range(2)]
        h_scale = [held("h_scale%d" % h, [P, HALF], U8) for h in range(2)]

        nc.gpsimd.memset(warm_in[:], 0.0)
        nc.scalar.activation(warm_out[:], warm_in[:], GELU)
        for m in range(2):
            nc.gpsimd.memset(w_scale[m][:].bitcast(I32), 0)
        nc.gpsimd.memset(wd_scale[:].bitcast(I32), 0)
        make_identity(nc, ident[:])

        def load_scales(m, q):
            scales = (wg_scales, wu_scales)[m]
            nc.sync.dma_start(
                w_scale[m][32 * q : 32 * q + 4, :].bitcast(I32).rearrange("r (a c) -> r a c", a=PASSES),
                scales.bitcast(I32)[:, 4 * q : 4 * q + 4, :].rearrange("a r c -> r a c"),
            )

        def load_down_scales(q):
            nc.sync.dma_start(
                wd_scale[32 * q : 32 * q + 4, :].bitcast(I32), wd_scales[0].bitcast(I32)[4 * q : 4 * q + 4, :]
            )

        def load_plane(s):
            a, i = divmod(s, PACK)
            rows = xT[P * PACK * a : P * PACK * (a + 1), :].rearrange("(p i) t -> p i t", i=PACK)
            nc.sync.dma_start(planes[s][:], rows[:, i, :])

        def load_words(m, a):
            words = (wg_words, wu_words)[m]
            nc.sync.dma_start(w_codes[m][a], words[a].rearrange("p r i -> p (r i)").bitcast(I32))

        last = PASSES * PACK - 1
        wgt_rows = held("wgt_rows", [P, J // LANES], F32)
        nc.sync.dma_start(wgt_rows[:], wgt[0:P:LANES, :].rearrange("g (c s) -> g c s", c=LANES))
        load_plane(0)
        nc.sync.dma_start(picks[:], offs)
        for s in range(1, last):
            load_plane(s)
            if s < PACK:
                load_scales(0, s - 1)
                load_down_scales(s - 1)
            if s == PACK + 1:
                load_down_scales(3)
                load_scales(0, 3)
        load_words(0, 0)
        load_plane(last)

        def load_the_rest():
            for q in range(4):
                load_scales(1, q)
            load_words(1, 0)
            load_words(0, 1)
            load_words(1, 1)
            nc.sync.dma_start(wd_codes[:].bitcast(I32), wd_words[0].bitcast(I32))
            with nc.allow_non_contiguous_dma(reason="one bias value a partition and output tile"):
                nc.sync.dma_start(bias[:], b.rearrange("(t p) -> p t", p=P))
            nc.sync.dma_start(places[:], offs2)
            for h in range(2):
                nc.sync.dma_start(wgo_sb[h][:], wgo[:, h * HALF : (h + 1) * HALF])

        SQUARE = 32
        wgt_turned = held("wgt_turned", [P, 2, SQUARE], F32)
        for u in range(2):
            nc.vector.transpose(wgt_turned[:, u, :], wgt_rows[:, u * SQUARE : (u + 1) * SQUARE])
        by_block = wgt_turned[:].rearrange("p u (e c) -> p c u e", e=2)
        for k in range(4):
            spread = held("spread%d" % k, [P, 4, 2, 2, LANES], F32)
            source = by_block[:, 4 * k : 4 * k + 4].unsqueeze(4).to_broadcast([P, 4, 2, 2, LANES])
            if k % 2:
                nc.vector.tensor_copy(spread[:], source)
            else:
                nc.scalar.copy(spread[:], source)
            nc.vector.transpose(
                wgt_sb[:, k * J // 4 : (k + 1) * J // 4], spread[:].rearrange("p c u e r -> p (c u e r)")
            )

        windows = [held("window%d" % t, [P, T], F32, after="spread%d" % t) for t in range(N_TILES)]
        for t in range(N_TILES):
            nc.gpsimd.memset(windows[t][:].bitcast(I32), 0)

        def gather(dst, s, j0, j1):
            nc.vector.tensor_tensor(
                dst, planes[s][:].indirect(picks[:, j0 // LANES : j1 // LANES]), wgt_sb[:, j0:j1], MULT
            )

        def interleave(dst, src):
            nc.scalar.copy(dst, src.rearrange("p i j -> p j i"))

        def quantize(codes, scales, grouped):
            nc.vector.quantize_mx(out=codes.bitcast(FP8X4), scales=scales, in_=grouped.rearrange("p j i -> p (j i)"))

        def first_layer(acc, m, a, h, c):
            piece, j0 = (2 + c // 2, c % 2 * CHUNK) if a == h == 1 else (h, c * CHUNK)
            nc.tensor.matmul_mx(
                out=acc[:],
                lhsT=x_codes[a, piece][:, j0 : j0 + CHUNK].bitcast(FP8X4),
                lhsT_scale=x_scale[a, piece][:, j0 : j0 + CHUNK],
                rhs=w_codes[m][a].bitcast(FP8X4),
                rhs_scale=w_scale[m][:, a * R : (a + 1) * R],
                start=(a == 0),
                stop=(a == PASSES - 1),
            )

        def gate(act, ga):
            nc.scalar.activation(act, ga[:], GELU)

        def product(hid, act, ub):
            nc.vector.tensor_tensor(hid, ub[:], act, MULT)

        def transposes(hid, index, dst):
            turned = bank(index, [P, 2, CHUNK])
            words = hid.bitcast(F32)
            for u in range(2):
                nc.tensor.transpose(turned[:, u, :], words[:, u : 2 * P : 2], ident[:])
            return dst.bitcast(F32), turned[:].rearrange("p u j -> p j u")

        def down(h, t, c0, c1, index):
            acc = bank(index, [P, c1 - c0])
            nc.tensor.matmul_mx(
                out=acc[:],
                lhsT=wd_codes[:, 2 * P * t : 2 * P * (t + 1)].bitcast(FP4X4),
                lhsT_scale=wd_scale[:, P * t : P * (t + 1)],
                rhs=h_codes[h][:, c0:c1].bitcast(FP8X4),
                rhs_scale=h_scale[h][:, c0:c1],
                start=True,
                stop=True,
            )
            return acc[:]

        def target(h, t, c0, c1):
            j0, j1 = h * HALF + c0, h * HALF + c1
            return windows[t][:].indirect(places[:, j0 // LANES : j1 // LANES])

        def biased(y, acc, t):
            nc.scalar.activation(y, acc, IDENTITY, bias=bias[:, t : t + 1])

        def weighed_on_vector(h, t, c0, c1, acc, after=None):
            y = held("y%d%d%d" % (h, t, c0), [P, c1 - c0], F32, after=after)
            nc.vector.scalar_tensor_tensor(
                y[:], acc, bias[:, t : t + 1], wgo_sb[h][:, c0:c1], mybir.AluOpType.add, MULT
            )
            return y

        def weigh_on_gpsimd(weighed, y, h, c0, c1):
            nc.gpsimd.tensor_tensor(weighed, y, wgo_sb[h][:, c0:c1], MULT)

        def place(h, t, c0, c1, weighed):
            nc.vector.tensor_copy(target(h, t, c0, c1), weighed)

        def weigh_and_place(h, t, c0, c1, y):
            nc.vector.tensor_tensor(target(h, t, c0, c1), y, wgo_sb[h][:, c0:c1], MULT)

        QUARTER = HALF // 2

        def as_grouped(rows):
            return rows.bitcast(BF16).rearrange("p (j i) -> p j i", i=PACK)

        first_pass = [held("first_pass%d" % u, [P, 2, J], F32) for u in range(2)]
        grouped0 = held("grouped0", [P, J, PACK], BF16)
        for s in range(PACK):
            gather(first_pass[s // 2][:, s % 2, :], s, 0, J)
            if s % 2:
                for h in range(2):
                    cols = slice(h * HALF, (h + 1) * HALF)
                    interleave(grouped0[:, cols, s - 1 : s + 1], first_pass[s // 2][:, :, cols])

        parts = ((0, CHUNK), (CHUNK, 2 * CHUNK), (2 * CHUNK, HALF))
        early = held("early", [P, 2, J], F32)
        grouped1 = [held("grouped1%d" % n, [P, c1 - c0, PACK], BF16) for n, (c0, c1) in enumerate(parts)]
        grouped_late = [held("grouped_late%d" % k, [P, QUARTER, PACK], BF16) for k in range(2)]
        codes0 = held("x_codes0", [P, J], I32)

        def first_pass_quantize(h):
            cols = slice(h * HALF, (h + 1) * HALF)
            x_codes[0, h], x_scale[0, h] = codes0[:, cols], (wd_scale[4:, :], w_scale[0][4:, R:])[h]
            quantize(x_codes[0, h], x_scale[0, h], grouped0[:, cols, :])

        gather(early[:, 0, :], PACK, 0, J)
        for h in range(2):
            gather(early[:, 1, h * HALF : (h + 1) * HALF], PACK + 1, h * HALF, (h + 1) * HALF)
            first_pass_quantize(h)
        load_the_rest()
        for n, (c0, c1) in enumerate(parts):
            interleave(grouped1[n][:, :, 0:2], early[:, :, c0:c1])
        for k in range(2):
            c0 = HALF + k * QUARTER
            interleave(grouped_late[k][:, :, 0:2], early[:, :, c0 : c0 + QUARTER])
        x_codes[1, 0] = held("x_codes10", [P, HALF], I32)[:]
        x_scale[1, 0] = held("x_scale10", [P, HALF], U8)[:]
        last_two = held("last_two", [P, 2 * HALF + QUARTER], F32)
        pair_last = last_two[:, 0 : 2 * HALF].rearrange("p (i j) -> p i j", i=2)
        gather(pair_last[:, 0, :], last - 1, 0, HALF)
        ga = [bank(2 * c, [P, R]) for c in range(CHUNKS)]
        ub = [bank(2 * c + 1, [P, R]) for c in range(CHUNKS)]
        for c in range(CHUNKS):
            first_layer(ga[c], 0, 0, 0, c)

        for n, (c0, c1) in enumerate(parts):
            gather(pair_last[:, 1, c0:c1], last, c0, c1)
        acts = [held("act%d" % c, [P, R], F32)[:] for c in range(CHUNKS)]
        hids = [
            last_two[:, CHUNK : CHUNK + QUARTER].bitcast(BF16),
            held("hid1", [P, R], BF16)[:],
            last_two[:, 2 * HALF :].bitcast(BF16),
            held("hid3", [P, R], BF16)[:],
        ]
        h_first = [held("h_first%d" % k, [P, QUARTER, PACK], BF16) for k in range(2)]

        def x_part(n):
            c0, c1 = parts[n]
            interleave(grouped1[n][:, :, 2:4], pair_last[:, :, c0:c1])
            quantize(x_codes[1, 0][:, c0:c1], x_scale[1, 0][:, c0:c1], grouped1[n][:])

        late = [pair_last[:, :, 0:QUARTER], last_two[:, HALF + QUARTER :].rearrange("p (i j) -> p i j", i=2)]

        def late_gather(k, i, c0, c1):
            j0 = HALF + k * QUARTER
            gather(late[k][:, i, c0:c1], last - 1 + i, j0 + c0, j0 + c1)

        def late_interleave(k):
            interleave(grouped_late[k][:, :, 2:4], late[k])

        def first_transposes(c, index):
            return transposes(hids[c], index, h_first[c // 2][:, (c % 2) * CHUNK : (c % 2 + 1) * CHUNK, :])

        def first_turn(c, index):
            nc.scalar.copy(*first_transposes(c, index))

        def late_quantize(k, after=None):
            x_codes[1, 2 + k] = held("x_codes_late%d" % k, [P, QUARTER], I32, after=after)[:]
            x_scale[1, 2 + k] = held("x_scale_late%d" % k, [P, QUARTER], U8)[:]
            quantize(x_codes[1, 2 + k], x_scale[1, 2 + k], grouped_late[k][:])

        first_layer(ub[0], 1, 0, 0, 0)
        first_layer(ub[1], 1, 0, 0, 1)
        x_part(0)
        first_layer(ga[0], 0, 1, 0, 0)
        first_layer(ub[2], 1, 0, 0, 2)
        late_gather(0, 0, 0, CHUNK)
        x_part(1)
        first_layer(ga[1], 0, 1, 0, 1)
        first_layer(ub[0], 1, 1, 0, 0)
        first_layer(ub[1], 1, 1, 0, 1)
        first_layer(ub[3], 1, 0, 0, 3)
        late_gather(0, 1, 0, QUARTER)
        x_part(2)
        late_gather(1, 0, 0, QUARTER)
        for c in (2, 3):
            first_layer(ga[c], 0, 1, 0, c)
            first_layer(ub[c], 1, 1, 0, c)
        for c in range(CHUNKS):
            gate(acts[c], ga[c])
        product(hids[0], acts[0], ub[0])
        product(hids[1], acts[1], ub[1])
        first_turn(0, 0)
        first_turn(1, 2)
        product(hids[2], acts[2], ub[2])
        late_gather(0, 0, CHUNK, QUARTER)
        product(hids[3], acts[3], ub[3])
        late_interleave(0)
        quantize(h_codes[0][:, 0:QUARTER], h_scale[0][:, 0:QUARTER], h_first[0][:])
        hand_over = first_transposes(2, 0)
        late_gather(1, 1, 0, QUARTER)
        nc.vector.tensor_copy(*hand_over)
        first_turn(3, 2)
        accs = [down(0, t, 0, QUARTER, index) for t, index in enumerate((4, 6))]
        late_quantize(0)
        first0 = weighed_on_vector(0, 0, 0, QUARTER, accs[0])
        quantize(h_codes[0][:, QUARTER:HALF], h_scale[0][:, QUARTER:HALF], h_first[1][:])
        late_interleave(1)
        y1 = held("y01a", [P, QUARTER], F32)
        biased(y1[:], accs[1], 1)
        first1 = held("weighed01a", [P, QUARTER], F32, after="h_first1")
        weigh_on_gpsimd(first1[:], y1[:], 0, 0, QUARTER)
        place(0, 0, 0, QUARTER, first0[:])
        late_quantize(1)
        place(0, 1, 0, QUARTER, first1[:])

        banks = ((0, 2), (4, 6), (5, 7), (1, 3))
        ga, ub = {}, {}

        def second_first_layer(c):
            ga[c], ub[c] = bank(banks[c][0], [P, R]), bank(banks[c][1], [P, R])
            for a in range(PASSES):
                first_layer(ga[c], 0, a, 1, c)
                first_layer(ub[c], 1, a, 1, c)

        act_pairs = [held("act_pair%d" % k, [P, 2, R], F32, after="plane%d" % k) for k in range(2)]
        up_flat = [held("up_pair%d" % k, [P, 2 * R + HALF - CHUNK], F32, after="plane%d" % (2 + k)) for k in range(2)]
        up_pairs = [flat[:, 0 : 2 * R].rearrange("p (k r) -> p k r", k=2) for flat in up_flat]

        def leave_banks(c):
            gate(act_pairs[c // 2][:, c % 2, :], ga[c])
            nc.scalar.copy(up_pairs[c // 2][:, c % 2, :], ub[c][:])

        y2 = held("y02", [P, HALF], F32)
        biased(y2[:], down(0, 2, 0, HALF, 5), 2)
        weighed2 = held("weighed02", [P, HALF], F32, after="grouped_late1")
        weigh_on_gpsimd(weighed2[:], y2[:], 0, 0, HALF)
        place(0, 2, 0, HALF, weighed2[:])
        accs = [down(0, t, QUARTER, HALF, index) for t, index in enumerate((7, 1))]
        ys = held("y0b", [P, 2, QUARTER], F32)
        weighed = held("weighed0b", [P, 2, QUARTER], F32)
        for t in range(2):
            biased(ys[:, t, :], accs[t], t)
        both = wgo_sb[0][:, QUARTER:HALF].unsqueeze(1).to_broadcast([P, 2, QUARTER])
        nc.gpsimd.tensor_tensor(weighed[:], ys[:], both, MULT)
        for t in range(2):
            place(0, t, QUARTER, HALF, weighed[:, t, :])
        for c in range(CHUNKS):
            second_first_layer(c)
            leave_banks(c)
        acc3 = down(0, 3, 0, HALF, 5)
        hid_second = held("hid_second", [P, CHUNKS, R], BF16, after="y02")
        hids = [hid_second[:, c, :] for c in range(CHUNKS)]
        h_second = [held("h_second%d" % k, [P, QUARTER, PACK], BF16) for k in range(2)]

        def second_turn(c, index):
            nc.scalar.copy(*transposes(hids[c], index, h_second[c // 2][:, (c % 2) * CHUNK : (c % 2 + 1) * CHUNK, :]))

        for k in range(2):
            nc.gpsimd.tensor_tensor(hid_second[:, 2 * k : 2 * k + 2, :], up_pairs[k], act_pairs[k][:], MULT)
        second_turn(0, 2)
        second_turn(1, 4)
        quantize(h_codes[1][:, 0:QUARTER], h_scale[1][:, 0:QUARTER], h_second[0][:])
        second_turn(2, 6)
        y3 = up_flat[1][:, 2 * R - CHUNK :]
        biased(y3[:, CHUNK:], acc3[:, CHUNK:], 3)
        biased(y3[:, 0:CHUNK], acc3[:, 0:CHUNK], 3)
        weigh_and_place(0, 3, 0, HALF, y3)
        second_turn(3, 7)
        quantize(h_codes[1][:, QUARTER:HALF], h_scale[1][:, QUARTER:HALF], h_second[1][:])
        y0 = held("y10a", [P, QUARTER], F32)
        biased(y0[:], down(1, 0, 0, QUARTER, 7), 0)
        weigh_and_place(1, 0, 0, QUARTER, y0[:])
        y1 = held("y11", [P, HALF], F32)
        biased(y1[:, 0:QUARTER], down(1, 1, 0, QUARTER, 6), 1)
        biased(y1[:, QUARTER:HALF], down(1, 1, QUARTER, HALF, 4), 1)
        weigh_and_place(1, 1, 0, HALF, y1[:])
        nc.sync.dma_start(out[P : 2 * P, :], windows[1][:])
        for t, c0, index in ((0, QUARTER, 0), (2, 0, 1), (3, 0, 2)):
            y = held("y1%d%d" % (t, c0), [P, HALF - c0], F32)
            biased(y[:], down(1, t, c0, HALF, index), t)
            weigh_and_place(1, t, c0, HALF, y[:])
            if t < N_TILES - 1:
                nc.sync.dma_start(out[P * t : P * (t + 1), :], windows[t][:])
        for queue, c0 in ((nc.sync, 0), (nc.scalar, T // 2)):
            queue.dma_start(out[N - P : N, c0 : c0 + T // 2], windows[N_TILES - 1][:, c0 : c0 + T // 2])
